import numpy as np, ml_dtypes
CORES = [35,38,43,46]
N = 4
BF = ml_dtypes.bfloat16
def gentries(a):
    return np.ascontiguousarray(a.reshape(8, 16, -1).transpose(0, 2, 1)).reshape(8, -1)
def gtable(e):
    e = np.asarray(e); return np.ascontiguousarray(e.reshape(8, -1, 16).transpose(0, 2, 1)).reshape(128, -1).astype(np.int32)
C, L, HOPS = 1024, 4, (1, 1, 1, 1, 1, 1, 1, 1)
W = C * L; RO = len(HOPS); B = 2 ** RO; NB = C // B
def lay(rng):
    P = np.argsort(rng.random((8, W)), axis=-1)
    for g in range(8):
        for k, v in ((W - 1, W - 1), (W - 2, 0)):
            j = int(np.flatnonzero(P[g] == v)[0]); P[g, j] = P[g, k]; P[g, k] = v
    return P.reshape(8, NB, B, L)
def turned(rng, P):
    ix = (np.arange(L) + rng.integers(0, L, (N, NB, B))[..., None]) % L
    return np.array(np.take_along_axis(np.broadcast_to(P, (N,) + P.shape), np.broadcast_to(ix[:, None], (N,) + P.shape), -1))
def mix(rng, e, b):
    for q in range(N):
        for g in range(8): e[q, g, b] = rng.permutation(e[q, g, b].reshape(-1)).reshape(B, L)
def pack(e, x):
    return {"o": np.stack([gtable(a) for a in e.reshape(N, 8, W)]), "x": np.ascontiguousarray(x.reshape(N, 128, W)).astype(np.float32).astype(BF)}
def place(P, v):
    inv = np.argsort(P.reshape(8, W), axis=-1)
    return np.take_along_axis(v.reshape(N, 8, 16, W), np.broadcast_to(inv[None, :, None, :], (N, 8, 16, W)), -1)
def parity():
    return np.array([bin(i).count("1") % 2 for i in range(B)])
def setup_inputs(rng):
    return pack(np.argsort(rng.random((N, 8, W)), axis=-1), rng.integers(0, 16, (N, 8, 16, W)))
def setup_inputs_spread(rng):
    hi = rng.integers(1, 17, (N, 8, 1, W)) * (rng.random((N, 8, 1, W)) > 0.0625)
    v = np.floor(hi * rng.random((N, 8, 16, W)) ** rng.choice(np.array([0.5, 1.0, 2.0, 4.0]), (N, 8, 16, 1)))
    return pack(np.argsort(rng.random((N, 8, W)), axis=-1), v)
def setup_inputs_ends(rng):
    P = lay(rng); e = turned(rng, P); v = 15 * rng.integers(0, 2, (N, 8, 16, NB, B, L)); flip = rng.integers(0, 2, (N, 1, 1, 1, 1)); par = parity()[:, None]
    for b in range(NB):
        k = (NB - 1 - b) % 4
        if k == 2: mix(rng, e, b); continue
        v[:, :, :, b] = 15 * ((par if k != 1 else 0 * par) ^ flip)
        if k < 2: v[:, 7, 15, b] = np.where(rng.random((N, B, L)) < 0.5, 15 - v[:, 7, 15, b], v[:, 7, 15, b])
    return pack(e, place(P, v))
def setup_inputs_edge(rng):
    P = lay(rng); e = turned(rng, P); v = rng.integers(0, 2, (N, 8, 16, NB, B, L)); flip = rng.integers(0, 2, (N, 1, 1, 1, 1)); par = parity()[:, None]
    for b in range(NB):
        k = (NB - 1 - b) % 4
        if k == 0:
            v[:, :, :, b] = 15 * (par ^ flip); v[:, 7, 15, b] = rng.integers(7, 10, (N, B, L))
        if k == 1:
            h = rng.integers(0, 15, (N, 8, 16, 1, L // 2)); v[:, :, :, b] = h[..., np.arange(L) % (L // 2)]
            v[:, 0, 0, b, :, 0] += rng.integers(0, 2, (N, B))
        if k == 2: mix(rng, e, b)
        if k == 3: v[:, :, :, b] = rng.integers(0, 16, (N, 8, 16, B, 1))
    return pack(e, place(P, v))
def setup_inputs_gap(rng):
    P = lay(rng); e = turned(rng, P); v = np.zeros((N, 8, 16, NB, B, L), np.int64); flip = rng.integers(0, 2, (N, 1, 1, 1, 1)); par = parity()[:, None]
    col = np.arange(L)[None, :]; z = int(rng.integers(0, 4))
    for b in range(NB):
        k = (NB - 1 - b) % 4
        if k == 0 or k == 3:
            v[:, :, :, b] = 15 * ((col % 2 if k == 0 else col // (L // 2)) ^ flip)
            v[:, 7, 15, b] = np.abs(v[:, 7, 15, b] - rng.integers(0, 2, (N, B, L)))
        if k == 1:
            for q in range(N):
                fl = int(flip[q, 0, 0, 0, 0]); u = 15 * ((col % 2) ^ (0 * par) ^ fl); w = 15 * ((col % 2) ^ par ^ fl)
                for m in range(8):
                    g = (m + 2 * (q + z)) % 8
                    if m < 3: v[q, g, :, b] = w
                    if m == 3 or m == 6: v[q, g, :, b] = u
                    if m == 4 or m == 5:
                        for i in rng.permutation(16)[:8]: v[q, g, int(i), b] = u
                    if m == 7: v[q, g, :, b] = rng.integers(0, 16, (16, B, 1))
        if k == 2:
            v[:, :, :, b] = 15 * (par ^ flip)
            up = par ^ flip[:, 0, 0]; h = rng.integers(1, 16, (N, 1, 1))
            v[:, 7, 15, b] = np.where(np.arange(L) == rng.integers(0, L, (N, B, 1)), h - up, 15 * up)
    return pack(e, place(P, v))
def setup_inputs_corners(rng):
    one = np.arange(W); e = np.argsort(rng.random((N, 8, W)), axis=-1)
    for g in range(8):
        both = rng.permutation(W)
        for q in range(N):
            h = (g + 2 * (q % 2)) % 8
            if h == 0: e[q, g] = one
            if h == 1: e[q, g] = one[::-1]
            if h == 2: e[q, g] = np.roll(one, 1)
            if h == 3: e[q, g] = both
            if h == 4: e[q, g] = one.reshape(L, C).T.reshape(-1)
            if h == 5: e[q, g] = np.argsort(both)
            if h == 6: e[q, g] = np.roll(one.reshape(C, L), q + 1, axis=1).reshape(-1)
    x = rng.integers(0, 16, (N, 8, 16, W)); w = rng.permutation(N)
    x[w[0]] = 15; x[w[1], :7] = 0; x[w[2], ::2] = 15 * rng.integers(0, 2, (4, 16, W))
    return pack(e, x)
def check_inputs(d):
    bad = []; v = np.asarray(d["x"]).astype(np.float32); c = np.asarray(d["o"])
    if not np.all((v >= 0) & (v <= 15)): bad.append("range of x")
    if not np.all(v == np.floor(v)): bad.append("whole numbers of x")
    if np.min(c) < 0 or np.max(c) > W - 1: bad.append("range of o")
    if np.any(np.sort(np.stack([gentries(a) for a in c]), axis=-1) != np.arange(W)): bad.append("permutation of o")
    return bad
def reference(o, x):
    cy = np.stack([gentries(a) for a in o]).astype(np.int64)
    xv = x.astype(np.float32).astype(np.int32).reshape(N, 8, 16, W); num = np.arange(C)
    for t in range(RO):
        lo = num[(num >> t) % 2 == 0]; hi = lo + 2 ** t; roots = []
        for q in range(N):
            cq = cy[q].reshape(8, C, L); a = cq[:, lo]; b = cq[:, hi]
            xa = np.take_along_axis(xv[q], a.reshape(8, 1, -1), 2).reshape(128, C // 2, L)
            xb = np.take_along_axis(xv[q], b.reshape(8, 1, -1), 2).reshape(128, C // 2, L)
            score = np.stack([np.add.reduce(np.abs(xa - np.roll(xb, -k, axis=2)), axis=(0, 2)) for k in range(L)])
            s = np.argmin(score, axis=0)
            ix = np.broadcast_to((np.arange(L)[None, :] + s[:, None]) % L, b.shape)
            bs = np.take_along_axis(b, ix, 2)
            f = np.zeros((8, W), np.int64)
            np.put_along_axis(f, a.reshape(8, -1), bs.reshape(8, -1), 1)
            np.put_along_axis(f, bs.reshape(8, -1), np.roll(a, -1, axis=2).reshape(8, -1), 1)
            roots.append(f)
        cy = np.stack([np.take_along_axis(roots[(r - HOPS[t]) % N], cy[r], 1) for r in range(N)])
    return {"yo": np.stack([gtable(e) for e in cy]).astype(np.float32)}

@@ -1,0 +1,619 @@
+from concourse.mybir import dt, AluOpType, AxisListType, ActivationFunctionType
+
+RO = 8
+EPS = 2.0 ** -14
+CFG = {"side": 0, "g0": 2, "g1": 0, "g2": 3}
+
+
+def _ta_shape(t):
+    if t == 1:
+        return [128, 4, 32, 2]
+    if 2 <= t <= 6:
+        tb = t - 2
+        return [128, 4, 2, 2 ** (4 - tb), 2, 2 ** tb]
+    return [128, 4, 2, 32]
+
+
+def _msg_shape(t):
+    if t < 2:
+        return [128, 4, 64]
+    tb = t - 2
+    return [128, 4, 2 ** (5 - tb), 2, 2 ** tb]
+
+
+SCRATCH = {
+    "U": ("sbuf", [128, 4096], "float32"),
+    "Y": ("sbuf", [128, 4096], "float32"),
+    "F": ("sbuf", [128, 4096], "float32"),
+    "B": ("sbuf", [128, 4096], "float32"),
+    "Z": ("sbuf", [128, 4096], "float32"),
+    "xb": ("sbuf", [128, 4096], "bfloat16"),
+    "mx0": ("sbuf", [128, 128, 4, 4], "bfloat16"),
+    "mx1": ("sbuf", [128, 128, 4, 4], "bfloat16"),
+    "zb": ("sbuf", [128, 1024], "bfloat16"),
+    "oi": ("sbuf", [128, 256], "int32"),
+    "LA": ("sbuf", [128, 256], "uint16"),
+    "XT": ("sbuf", [128, 2, 2, 128], "bfloat16"),
+    "X1": ("sbuf", [128, 2, 128], "bfloat16"),
+    "CT": ("sbuf", [128, 2, 128], "float32"),
+    "cn": ("sbuf", [128, 128], "float32"),
+    "Tb": ("sbuf", [128, 2, 2, 128], "float32"),
+    "xib": ("sbuf", [128, 2, 2, 128], "bfloat16"),
+    "Tt": ("sbuf", [128, 2, 8, 32], "float32"),
+    "UT": ("sbuf", [128, 2, 2, 128], "float32"),
+    "Tc": ("sbuf", [128, 4, 2, 32], "float32"),
+    "xia": ("sbuf", [128, 4, 2, 32], "bfloat16"),
+    "sel": ("sbuf", [128, 3 * 144], "bfloat16"),
+    "tie": ("sbuf", [128, 128], "bfloat16"),
+    "srow": ("sbuf", [128, 256], "bfloat16"),
+    "rst": ("sbuf", [128, 256], "float32"),
+    "one": ("sbuf", [128, 128], "float32"),
+    "big": ("sbuf", [128, 128], "float32"),
+    "e14": ("sbuf", [128, 128], "float32"),
+    "I14": ("sbuf", [128, 128], "float32"),
+    "nI": ("sbuf", [128, 128], "bfloat16"),
+    "pI": ("sbuf", [128, 128], "bfloat16"),
+    "rot": ("sbuf", [128, 8, 32, 4], "float32"),
+    "pm0": ("sbuf", [128, 4, 16, 2, 4], "float32"),
+    "pm1": ("sbuf", [128, 4, 8, 2, 2, 4], "float32"),
+    "RM0": ("sbuf", [128, 256], "float32"),
+    "RM1": ("sbuf", [128, 256], "float32"),
+    "E": ("sbuf", [128, 1024], "float32"),
+    "D": ("sbuf", [128, 1024], "float32"),
+    "SL": ("sbuf", [128, 1024], "int32"),
+    "UP": ("sbuf", [128, 2, 128], "int32"),
+    "pA0": ("psum", [128, 512], "float32"),
+    "pA1": ("psum", [128, 512], "float32"),
+    "pK0": ("psum", [128, 512], "float32"),
+    "pK1": ("psum", [128, 512], "float32"),
+    "pP0": ("psum", [128, 512], "float32"),
+    "pP1": ("psum", [128, 512], "float32"),
+    "pE": ("psum", [128, 8, 2, 2, 16], "float32"),
+    "pB": ("psum", [128, 2, 8, 2, 16], "float32"),
+}
+for _t in range(RO + 1):
+    SCRATCH["Ta%d" % _t] = ("sbuf", _ta_shape(_t), "float32")
+for _t in range(RO):
+    SCRATCH["MS%d" % _t] = ("sbuf", _msg_shape(_t), "uint16")
+    SCRATCH["LM%d" % _t] = ("sbuf", [128, 256], "uint16")
+    SCRATCH["BS%d" % _t] = ("sbuf", [128, 2, 32, 8], "uint16")
+    SCRATCH["LB%d" % _t] = ("sbuf", [128, 512], "uint16")
+SCRATCH["Lm1"] = ("sbuf", [128, 4, 2, 32], "uint16")
+for _t in range(2, 7):
+    SCRATCH["Lm%d" % _t] = ("sbuf", _ta_shape(_t), "uint16")
+
+SEMAPHORES = ["v", "s", "p", "gc", "ls", "d_o", "d_x", "d_xt", "d_c", "d_cb", "d_ex", "d_rl", "d_out", "d_cast"]
+SEMAPHORES += ["d_ca%d" % _k for _k in range(4)]
+SEMAPHORES += ["m%d_%d" % (_t, _k) for _t in range(RO) for _k in range(4)]
+SEMAPHORES += ["n%d_%d" % (_t, _k) for _t in range(RO) for _k in range(2)]
+
+
+def rank_program(g, core, T, topo):
+    rank = T.rank_of(core)
+    if rank is None:
+        return
+    A = AluOpType
+    AF = ActivationFunctionType
+    V, S, P = g.vector, g.scalar, g.tensor
+    n = len(T.cores)
+    dst = T.cores[(rank + 1) % n]
+    src = T.cores[(rank - 1) % n]
+    rid, pid, _se = topo.addr(dst)
+    mask = topo.mask(core, dst)
+    n_out = len(topo.engines(core, dst))
+    n_in = len(topo.engines(src, core))
+
+    queues = {"v": V, "s": S, "p": P, "y": g.sync, "g": g}
+    total = {}
+    waited = {q: {} for q in queues}
+    writer = {}
+    readers = {}
+
+    def need(q, reads, writes):
+        toks = []
+        for k in reads:
+            if k in writer:
+                toks.append(writer[k])
+        for k in writes:
+            if k in writer:
+                toks.append(writer[k])
+            toks.extend(readers.get(k, {}).items())
+        best = {}
+        for sem, cnt in toks:
+            if q == "p" and sem == "p":
+                continue
+            if sem.startswith("d_"):
+                cnt = total[sem]
+            best[sem] = max(best.get(sem, 0), cnt)
+        for sem, cnt in best.items():
+            if waited[q].get(sem, 0) < cnt:
+                queues[q].wait_ge(T.sem[sem], cnt)
+                waited[q][sem] = cnt
+
+    def done(tok, reads, writes):
+        for k in reads:
+            readers.setdefault(k, {})[tok[0]] = tok[1]
+        for k in writes:
+            writer[k] = tok
+            readers[k] = {}
+
+    def op(q, fn, reads, writes):
+        if q == "g":
+            writes = writes + ["pool"]
+        need(q, reads, writes)
+        sem = "gc" if q == "g" else q
+        fn().then_inc(T.sem[sem], 1)
+        total[sem] = total.get(sem, 0) + 1
+        done((sem, total[sem]), reads, writes)
+
+    def dmas(q, sem, pairs, reads, writes):
+        need(q, reads, writes)
+        for o_, i_ in pairs:
+            queues[q].dma_start(o_, i_).then_inc(T.sem[sem], 16)
+            total[sem] = total.get(sem, 0) + 16
+        done((sem, total[sem]), reads, writes)
+
+    def send(sem, o_, i_, reads, landed):
+        need("g", reads, [])
+        g.remote_dma(o_, i_, T.sem[sem], T.sem.ls, pid, rid, mask)
+        total["ls"] = total.get("ls", 0) + n_out
+        total[sem] = n_in
+        for k in landed:
+            writer[k] = (sem, n_in)
+
+    def pcs(name, a=0, b=8):
+        return [(name, k) for k in range(a, b)]
+
+    def gather(q, out, win, wkeys, lst, off, lkeys, a, b, add=None):
+        if a >= b:
+            return
+        o_ = T[out][:, 512 * a:512 * b]
+        i_ = T[win][:, 0:4096].indirect(T[lst][:, off + 32 * a:off + 32 * b])
+        if q == "v":
+            if add is None:
+                fn = lambda: V.tensor_copy(o_, i_)
+            else:
+                fn = lambda: V.tensor_scalar(o_, i_, add, None, A.add)
+        else:
+            fn = lambda: S.activation(o_, i_, AF.Identity, bias=(add or 0.0))
+        op(q, fn, wkeys + lkeys, pcs(out, a, b))
+
+    def copy(q, o_, i_, reads, writes):
+        if q == "v":
+            op(q, lambda: V.tensor_copy(o_, i_), reads, writes)
+        else:
+            op(q, lambda: S.activation(o_, i_, AF.Identity), reads, writes)
+
+    def pieces(d):
+        d %= 4
+        return [(0, 4 - d, d)] + ([(4 - d, d, 0)] if d else [])
+
+    def make_rot():
+        for h, ones in ((0, "one"), (1, "big")):
+            for d in range(4):
+                for j0, c, w0 in pieces(d):
+                    op("g", lambda: g.affine_select(T.rot[:, 4 * h + d, :, j0:j0 + c], T[ones][:, 0:32 * c], [[-4, 32], [-1, c]],
+                                                    A.is_equal, 0.0, -w0, 1), [ones], [("rot", h, d, j0)])
+
+    def make_pm(t):
+        for s in range(4):
+            for b in range(2):
+                for j0, c, w0 in pieces(s if b == 0 else 1 - s):
+                    if t == 0:
+                        fn = lambda: g.affine_select(T.pm0[:, s, :, b, j0:j0 + c], T.one[:, 0:16 * c], [[-8, 16], [-1, c]],
+                                                     A.is_equal, 0.0, -(4 * (1 - b) + w0), 1)
+                    else:
+                        fn = lambda: g.affine_select(T.pm1[:, s, :, b, :, j0:j0 + c], T.one[:, 0:16 * c],
+                                                     [[-16, 8], [-4, 2], [-1, c]], A.is_equal, 0.0, -(8 * (1 - b) + w0), 1)
+                    op("g", fn, ["one"], [("pm", t, s, b, j0)])
+
+    def rot_keys(h, d):
+        return [("rot", h, d, j0) for j0, _c, _w in pieces(d)]
+
+    def pm_keys(t, s):
+        return [("pm", t, s, b, j0) for b in range(2) for j0, _c, _w in pieces(s if b == 0 else 1 - s)]
+
+    def conv_b(parts):
+        dmas("y", "d_cb", [(T.Tb[:, w, h], T.B[16 * h + 2 * w::32, :]) for w in parts for h in range(2)], pcs("B"), ["Tb"])
+
+    def round_b(t):
+        copy("s", T.xib[:], T.Tb[:], ["Tb"], ["xib"])
+        if t < RO - 1:
+            op("p", lambda: P.matmul(T.pB[:], T.I14[:], T.Tb[:], True, False), ["I14", "Tb"], ["pB"])
+            op("p", lambda: P.matmul(T.pB[:], T.nI[:], T.xib[:], False, False), ["nI", "xib"], ["pB"])
+            op("p", lambda: P.matmul(T.pB[:], T.pI[:], T.XT[:], False, True), ["pI", "XT"], ["pB"])
+
+    def put_b(t):
+        if t < RO - 1:
+            op("s", lambda: S.activation(T.UT[:], T.pB[:], AF.Identity, scale=EPS), ["pB"], ["UT"])
+            dmas("y", "d_ex", [(T.U[16 * h + 2 * w::32, :], T.UT[:, w, h]) for w in range(2) for h in range(2)], ["UT"], ["U"])
+
+    def plain_b(i):
+        w, h = i // 2, i % 2
+        op("p", lambda: P.matmul(T.pB[:, w, :, h, :], T.I14[:], T.Tb[:, w, h], True, False), ["I14", "Tb"], ["pB"])
+        op("p", lambda: P.matmul(T.pB[:, w, :, h, :], T.nI[:], T.xib[:, w, h], False, True), ["nI", "xib"], ["pB"])
+
+    def list_b(t):
+        op("v", lambda: V.transpose(T.Tt[:], T.pB[:]), ["pB"], ["Tt"])
+        for r in range(8):
+            copy("v", T["BS%d" % t][:, :, :, r], T.Tt[:, :, r, :], ["Tt"], [("BS", t, r)])
+        keys = [("BS", t, r) for r in range(8)]
+        if t < RO - 1:
+            send("n%d_1" % t, T["LB%d" % t][:, 256:512], T["BS%d" % t][:, 1], keys, [("LB", t, 1)])
+        send("n%d_0" % t, T["LB%d" % t][:, 0:256], T["BS%d" % t][:, 0], keys, [("LB", t, 0)])
+
+    def conv_a(k):
+        dmas("y", "d_ca%d" % k, [(T.Tc[:, k, h], T.Z[16 * h + 1::32, 1024 * k:1024 * k + 1024]) for h in range(2)],
+             pcs("Z", 2 * k, 2 * k + 2), [("Tc", k)])
+
+    def round_a(k):
+        copy("s", T.xia[:, k], T.Tc[:, k], [("Tc", k)], [("xia", k)])
+        op("p", lambda: P.matmul(T.pE[:, k], T.I14[:], T.Tc[:, k], True, False), ["I14", ("Tc", k)], ["pE"])
+        op("p", lambda: P.matmul(T.pE[:, k], T.nI[:], T.xia[:, k], False, True), ["nI", ("xia", k)], ["pE"])
+
+    def low(t, k, r):
+        buf = T["Ta%d" % t]
+        if t == 1:
+            return buf[:, k, :, r]
+        if t == 2:
+            return buf[:, k, :, :, r, :]
+        if 2 < t <= 6:
+            return buf[:, k, :, :, :, r::2]
+        return buf[:, k, :, r::2]
+
+    def ta_keys(t, k0, k1):
+        return [("Ta", t, k, r) for k in range(k0, k1) for r in range(2)]
+
+    def turn_a(t, k):
+        for r in range(2):
+            op("v", lambda: V.transpose(low(t, k, r), T.pE[:, k, :, r, :]), ["pE"], [("Ta", t, k, r)])
+
+    def choices(t, u, shifts):
+        bank = "pP%d" % u
+        buf = T["Ta%d" % t]
+        k0, k1 = 2 * u, 2 * u + 2
+        for s in shifts:
+            if t < 2:
+                op("p", lambda: P.matmul(T[bank][:, s:512:4], T["pm%d" % t][:, s], buf[:, k0:k1], True, True),
+                   ta_keys(t, k0, k1) + pm_keys(t, s), [bank])
+            else:
+                d = (1 - s) % 4
+                op("p", lambda: P.matmul(T[bank][:, s:256:4], T.rot[:, 4 + s], buf[:, k0:k1, 1], True, False),
+                   ta_keys(t, k0, k1) + rot_keys(1, s), [bank])
+                op("p", lambda: P.matmul(T[bank][:, s:256:4], T.rot[:, d], buf[:, k0:k1, 0], False, True),
+                   ta_keys(t, k0, k1) + rot_keys(0, d), [bank])
+
+    def list_a(t):
+        buf = T["Ta%d" % t]
+        keys = ta_keys(t, 0, 4)
+        if t == 0:
+            return
+        if t == RO - 1:
+            copy("v", T.LA[:], buf[:], keys, ["LA"])
+            return
+        lm = T["Lm%d" % t]
+        if t == 1:
+            parts = [(lm[:, :, r, :], buf[:, :, :, r]) for r in range(2)]
+        else:
+            parts = [(lm[:, :, y, :, x, :], buf[:, :, x, :, y, :]) for x in range(2) for y in range(2)]
+        for i, (o_, i_) in enumerate(parts):
+            copy("v", o_, i_, keys, [("Lm", t, i)])
+        dmas("y", "d_rl", [(T.LA[:], lm[:])], [("Lm", t, i) for i in range(len(parts))], ["LA"])
+
+    def stage(q, t, k):
+        bank = "pA%d" % (k % 2)
+        z0 = 1024 * k
+        rd = pcs("Z", 2 * k, 2 * k + 2)
+        need(q, [], [bank])
+        if t >= 2:
+            copy(q, T[bank][:], T.Z[:, z0:z0 + 512], rd[:1], [bank])
+        elif t == 0:
+            for j in range(4):
+                copy(q, T[bank][:, 128 * j:128 * j + 128], T.Z[:, z0 + j:z0 + 1024:8], rd, [(bank, j)] if j < 3 else [bank])
+        else:
+            for j in range(4):
+                for o in range(2):
+                    copy(q, T[bank][:, 128 * j + o:128 * j + 128:2], T.Z[:, z0 + 4 * o + j:z0 + 1024:16], rd,
+                         [(bank, j, o)] if (j, o) != (3, 1) else [bank])
+
+    def scores(t, k, fill):
+        bank = "pA%d" % (k % 2)
+        kb = "pK%d" % (k % 2)
+        mname = "mx%d" % (k % 2)
+        mx = T[mname]
+        z0 = 1024 * k
+        rd = pcs("Z", 2 * k, 2 * k + 2) + [bank]
+        wd = 128 if t >= 2 else 256
+        fill = list(fill)
+        op("p", lambda: P.matmul(T[kb][:, 0:wd], T.tie[:], T.srow[:, 0:wd], True, False), ["tie", "srow"], [kb])
+        for j in range(4):
+            for s in range(4):
+                jj = (j + s) % 4
+                if t >= 2:
+                    op("v", lambda: V.tensor_tensor(mx[:, 32 * j:32 * j + 32, :, s], T[bank][:, j:512:4],
+                                                    T.Z[:, z0 + 512 + jj:z0 + 1024:4], A.max), rd, [(mname, j, s)])
+                elif t == 0:
+                    op("v", lambda: V.tensor_tensor(mx[:, 32 * j:32 * j + 32, :, s], T[bank][:, 128 * j:128 * j + 128],
+                                                    T.Z[:, z0 + 4 + jj:z0 + 1024:8], A.max), rd, [(mname, j, s)])
+                else:
+                    for o in range(2):
+                        op("v", lambda: V.tensor_tensor(mx[:, 32 * j:32 * j + 32, o::2, s], T[bank][:, 128 * j + o:128 * j + 128:2],
+                                                        T.Z[:, z0 + 8 + 4 * o + jj:z0 + 1024:16], A.max), rd,
+                           [(mname, j, s)] if o else [(mname, j, s, 0)])
+                if s % 2 == 1 and fill:
+                    fill.pop(0)()
+            sums(t, k, j)
+        for f in fill:
+            f()
+
+    def sums(t, k, j):
+        kb = "pK%d" % (k % 2)
+        mname = "mx%d" % (k % 2)
+        mx = T[mname]
+        keys = [(mname, j, s) for s in range(4)] + [(mname, j, s, 0) for s in range(4)] + ["sel"]
+        if t >= 2:
+            for o in range(4):
+                op("p", lambda: P.matmul(T[kb][:, 0:128], T.sel[:, 12 - 4 * o:140 - 4 * o], mx[:, 32 * j:32 * j + 32, o, :],
+                                         False, j == 3 and o == 3), keys, [kb])
+        else:
+            for o in range(2):
+                c0 = 144 + 8 - 8 * o if t == 0 else 288 + 4 - 4 * o
+                op("p", lambda: P.matmul(T[kb][:, 0:256], T.sel[:, c0:c0 + 128], mx[:, 32 * j:32 * j + 32, o::2, :],
+                                         False, j == 3 and o == 1), keys, [kb])
+
+    def side_scores(t, k):
+        kb = "pK%d" % (k % 2)
+        mname = "mx%d" % (k % 2)
+        mx = T[mname]
+        wd = 128 if t >= 2 else 256
+
+        def diff(j):
+            if j == 0:
+                copy("s", T.zb[:], T.Z[:, 1024 * k:1024 * k + 1024], pcs("Z", 2 * k, 2 * k + 2), ["zb"])
+            bank = "pA%d" % (k % 2) if j % 2 == 0 else "pB"
+            col = (lambda c, st: T[bank][:, c:512:st]) if j % 2 == 0 else (lambda c, st: T.pB[:, :, :, :, c::st])
+            for s in range(4):
+                jj = (j + s) % 4
+                if t >= 2:
+                    parts = [(col(s, 4), T.zb[:, j:512:4], T.zb[:, 512 + jj:1024:4])]
+                else:
+                    parts = [(col(4 * o + s, 8), T.zb[:, 4 * o + j:1024:16], T.zb[:, 8 + 4 * o + jj:1024:16]) for o in range(2)]
+                for o_, u_, w_ in parts:
+                    op("p", lambda: P.matmul(o_, T.pI[:], u_, True, False), ["pI", "zb"], [bank])
+                    op("p", lambda: P.matmul(o_, T.nI[:], w_, False, True), ["nI", "zb"], [bank])
+            op("s", lambda: S.activation(mx[:, 32 * j:32 * j + 32], T[bank][:], AF.Relu, scale=EPS), [bank],
+               [(mname, j, s) for s in range(4)] + [(mname, j, s, 0) for s in range(4)])
+
+        def keys(j):
+            if j == 0:
+                op("p", lambda: P.matmul(T[kb][:, 0:wd], T.tie[:], T.srow[:, 0:wd], True, False), ["tie", "srow"], [kb])
+            sums(t, k, j)
+
+        return [lambda j=j: diff(j) for j in range(4)], [lambda j=j: keys(j) for j in range(4)]
+
+    def least(t, k):
+        u = k % 2
+        kb = "pK%d" % u
+        wd = 128 if t >= 2 else 256
+        rm = T["RM%d" % u]
+        return [
+            lambda: op("v", lambda: V.tensor_tensor_scan(rm[:, 0:wd], T.rst[:, 0:wd], T[kb][:, 0:wd], 0.0, A.add, A.min),
+                       ["rst", kb], [("RM", u)]),
+            lambda: op("v", lambda: V.tensor_tensor(T.E[:, wd * k:wd * k + wd], T[kb][:, 0:wd], rm[:, 0:wd], A.subtract),
+                       [kb, ("RM", u)], [("E", k)]),
+        ]
+
+    def pick(t, k0, k1):
+        pb = "pP%d" % (k0 // 2)
+        wd = 128 if t >= 2 else 256
+        c0, c1 = wd * k0, wd * k1
+        p0 = wd * (k0 % 2)
+        ms = T["MS%d" % t]
+        ks = lambda name: [(name, k) for k in range(k0, k1)]
+        steps = [
+            lambda: op("v", lambda: V.tensor_tensor(T.D[:, c0:c1], T[pb][:, p0:p0 + c1 - c0], T.E[:, c0:c1], A.subtract),
+                       [pb] + ks("E"), ks("D")),
+            lambda: op("v", lambda: V.tensor_tensor_scan(T.SL[:, c0:c1], T.E[:, c0:c1], T.D[:, c0:c1], 0.0, A.min, A.max),
+                       ks("E") + ks("D"), ks("SL")),
+        ]
+
+        def unpack():
+            op("v", lambda: V.tensor_scalar(T.UP[:, 0, 32 * k0:32 * k1], T.SL[:, c0 + 3:c1:4], 12, None, A.logical_shift_right),
+               ks("SL"), ks("UP0"))
+            op("v", lambda: V.tensor_scalar(T.UP[:, 1, 32 * k0:32 * k1], T.SL[:, c0 + 3:c1:4], 4095, None, A.bitwise_and),
+               ks("SL"), ks("UP1"))
+
+        def out():
+            if t >= 2:
+                for b in range(2):
+                    copy("v", ms[:, k0:k1, :, b, :], T.UP[:, b, 32 * k0:32 * k1], ks("UP%d" % b), [("MS", t, k0, b)])
+            else:
+                copy("v", ms[:, k0:k1], T.SL[:, c0 + 3:c1:4], ks("SL"), [("MS", t, k0, 0)])
+            send("m%d_%d" % (t, k0), T["LM%d" % t][:, 64 * k0:64 * k1], ms[:, k0:k1],
+                 [("MS", t, k0, 0), ("MS", t, k0, 1)], [("LM", t, k) for k in range(k0, k1)])
+
+        if t >= 2:
+            steps.append(unpack)
+        steps.append(out)
+        return steps
+
+    def run(steps):
+        for f in steps:
+            f()
+
+    def ygather(q, t, a, b):
+        gather(q, "Y", "U", ["U"], "LM%d" % t, 0, [("LM", t, k) for k in range(a // 2, (b + 1) // 2)], a, b, 128.0)
+
+    def zgather(q, a, b):
+        gather(q, "Z", "F", pcs("F"), "LA", 0, ["LA"], a, b)
+
+    def bgather(q, t, a, b):
+        gather(q, "B", "Y", pcs("Y"), "LB%d" % (t - 1), 256, [("LB", t - 1, 1)], a, b)
+
+    def fgather(q, t, a, b):
+        gather(q, "F", "Y", pcs("Y"), "LB%d" % (t - 1), 0, [("LB", t - 1, 0)], a, b)
+
+    def tail(t):
+        list_a(t)
+        ygather("s" if t else "v", t, 0, 2)
+        ygather("s", t, 2, 4)
+        ygather("v", t, 4, 5)
+        ygather("s", t, 5, 6)
+        ygather("v", t, 6, 7)
+        ygather("s", t, 7, 8)
+
+    dmas("y", "d_o", [(T.oi[:], T.o[:])], [], ["oi"])
+    dmas("y", "d_x", [(T.xb[:, 0:2048], T.x[:, 0:2048])], [], ["xb"])
+    dmas("s", "d_x", [(T.xb[:, 2048:4096], T.x[:, 2048:4096])], [], ["xb2"])
+    copy("v", T.LA[:], T.oi[:], ["oi"], ["LA"])
+    for k in range(4):
+        op("g", lambda: g.iota(T.F[:, 1024 * k:1024 * k + 1024], [[1, 1024]], 128 + 1024 * k, 0, allow_small_or_imprecise_dtypes=True),
+           [], pcs("F", 2 * k, 2 * k + 2))
+        op("s", lambda: S.activation(T.B[:, 0:4096].indirect(T.LA[:, 64 * k:64 * k + 64]), T.F[:, 1024 * k:1024 * k + 1024], AF.Silu),
+           pcs("F", 2 * k, 2 * k + 2) + ["LA"], pcs("B"))
+    op("v", lambda: V.memset(T.one[:], 1.0), [], ["one"])
+    op("v", lambda: V.memset(T.e14[:], 16384.0), [], ["e14"])
+    dmas("y", "d_xt", [(T.XT[:, w, h], T.x[16 * h + 2 * w::32, :]) for w in range(2) for h in range(2)]
+         + [(T.X1[:, h], T.x[16 * h + 1::32, :]) for h in range(2)], [], ["XT", "X1"])
+    dmas("g", "d_cast", [(T.U[:], T.x[:])], [], ["U"])
+    make_pm(0)
+    op("g", lambda: g.affine_select(T.I14[:], T.e14[:], [[-1, 128]], A.is_equal, 0.0, 0, 1), ["e14"], ["I14"])
+    for h in range(4):
+        op("g", lambda: g.iota(T.cn[32 * h:32 * h + 32, :], [[1, 128]], 0, 128, allow_small_or_imprecise_dtypes=True), [], [("cn", h)])
+    cn = [("cn", h) for h in range(4)]
+    copy("v", T.Ta0[:], T.oi[:], ["oi"], ta_keys(0, 0, 4))
+    op("v", lambda: V.memset(T.big[:], 4096.0), [], ["big"])
+    op("v", lambda: V.memset(T.sel[:], 0.0), [], ["sel"])
+    op("v", lambda: V.memset(T.rst[:], 0.0), [], ["rst"])
+    op("v", lambda: V.memset(T.tie[:], 2.0 ** 17), [], ["tie"])
+    for s in range(4):
+        op("v", lambda: V.memset(T.srow[:, s:256:4], float(s)), [], [("srow", s)] if s < 3 else ["srow"])
+    need("v", ["sel", "rst"], [])
+    cols = [(12 + c, 144, 16) for c in range(4)] + [(152 + c, 288, 16) for c in range(8)] + [(292 + c, 432, 8) for c in range(4)]
+    for i, (c, end, step) in enumerate(cols):
+        op("v", lambda: V.memset(T.sel[:, c:end:step], 2.0 ** 26), [], [("sel", i)] if i < len(cols) - 1 else ["sel"])
+    op("v", lambda: V.memset(T.rst[:, 0:256:4], 2.0 ** 50), [], ["rst"])
+
+    def late_setup():
+        op("v", lambda: V.tensor_scalar(T.cn[:], T.cn[:], EPS, None, A.mult), cn, cn)
+        for h in range(2):
+            op("v", lambda: V.tensor_tensor(T.CT[:, h], T.X1[:, h], T.cn[:], A.add), cn + ["X1"], [("CT", h)])
+        dmas("y", "d_c", [(T.U[16 * h + 1::32, :], T.CT[:, h]) for h in range(2)], [("CT", 0), ("CT", 1)], ["U"])
+        op("v", lambda: V.tensor_scalar(T.nI[:], T.I14[:], -1.0, None, A.mult), ["I14"], ["nI"])
+        copy("v", T.pI[:], T.I14[:], ["I14"], ["pI"])
+
+    def first_b():
+        sl = T.SL[:, 768:1024]
+        ks = [("SL", 3)]
+        return [
+            lambda: op("v", lambda: V.tensor_scalar(sl, T.Tb[:, 0], -128.0, None, A.add), ["Tb"], ks),
+            lambda: op("v", lambda: V.tensor_scalar(sl, sl, 3, None, A.bitwise_and), ks, ks),
+            lambda: op("v", lambda: V.tensor_scalar(T.UT[:, 0], sl, 0.0, 4.0, A.is_equal, A.mult), ks, ["UT"]),
+            lambda: op("v", lambda: V.tensor_tensor(T.Tb[:, 1], T.Tb[:, 0], T.UT[:, 0], A.add), ["Tb", "UT"], ["Tb1"]),
+            lambda: (op("s", lambda: S.activation(T.Tb[:, 0], T.Tb[:, 0], AF.Identity, bias=128.0 - 128.0 * EPS, scale=EPS),
+                        ["Tb", "Tb1"], ["Tb"]),
+                     op("s", lambda: S.activation(T.Tb[:, 1], T.Tb[:, 1], AF.Identity, bias=128.0 - 129.0 * EPS, scale=EPS),
+                        ["Tb1"], ["Tb"]),
+                     round_b(0), put_b(0)),
+        ]
+
+    fill = []
+    for k in range(4):
+        gather("v", "Z", "xb", ["xb", "xb2"], "LA", 0, ["LA"], 2 * k, 2 * k + 2, 128.0)
+        stage("v", 0, k)
+        if k == 1:
+            late_setup()
+            conv_b([0])
+        if k == 3:
+            fb = first_b()
+            fill = fill[:2] + [lambda: run(fb[:2]), lambda: run(fb[2:])] + fill[2:]
+        scores(0, k, fill)
+        if k % 2 == 0:
+            choices(0, k // 2, range(4))
+        fill = least(0, k) + pick(0, k, k + 1)
+    for i in range(4):
+        plain_b(i)
+    run(fill)
+    list_b(0)
+    make_pm(1)
+    make_rot()
+    tail(0)
+
+    skip = lambda: None
+    both = lambda *fs: (lambda: run(fs))
+    for t in range(1, RO):
+        bgather("v", t, 0, 4)
+        bgather("s", t, 4, 8)
+        conv_b([0, 1])
+        fgather("v", t, 0, 4)
+        fgather("s", t, 4, 8)
+        lk = [least(t, k) for k in range(4)]
+        tr = [lambda k=k: turn_a(t, k) for k in range(4)]
+        ch = [[lambda u=u, s=s: choices(t, u, [s]) for s in range(4)] for u in range(2)]
+        p01, p2, p3 = pick(t, 0, 2), pick(t, 2, 3), pick(t, 3, 4)
+        zgather("v", 0, 1)
+        zgather("s", 2, 3)
+        if t < 2:
+            zgather("v", 1, 2)
+        stage("s", t, 0)
+        if t >= 2:
+            zgather("v", 1, 2)
+        conv_a(0)
+        zgather("s", 3, 4)
+        conv_a(1)
+        if not CFG["side"]:
+            round_b(t)
+            scores(t, 0, [])
+            stage("s", t, 1)
+            zgather("s", 4, 6)
+            conv_a(2)
+            put_b(t)
+            round_a(0)
+            scores(t, 1, [skip] * CFG["g2"] + lk[0] + [tr[0]])
+            round_a(1)
+            stage("s", t, 2)
+            zgather("s", 6, 8)
+            conv_a(3)
+            scores(t, 2, [both(tr[1], ch[0][0], ch[0][1]), lk[1][0], both(lk[1][1], ch[0][2], ch[0][3])] + [skip] * CFG["g0"] + p01)
+            stage("s", t, 3)
+            round_a(2)
+            scores(t, 3, [tr[2], lk[2][0], lk[2][1]] + [skip] * CFG["g1"]
+                   + [both(lambda: round_a(3), tr[3], ch[1][0], ch[1][1]), skip, both(ch[1][2], ch[1][3])])
+            for i in range(4):
+                plain_b(i)
+            run([p2[0], lk[3][0], p2[1], lk[3][1]] + p2[2:3] + [p3[0]] + p2[3:] + p3[1:])
+        else:
+            stage("s", t, 1)
+            scores(t, 0, [])
+            round_b(t)
+            zgather("s", 4, 6)
+            conv_a(2)
+            round_a(0)
+            round_a(1)
+            put_b(t)
+            zgather("s", 6, 8)
+            conv_a(3)
+            scores(t, 1, [skip] * CFG["g2"] + lk[0] + [tr[0], both(tr[1], ch[0][0], ch[0][1]), skip, both(ch[0][2], ch[0][3])])
+            stage("s", t, 2)
+            df, ky = side_scores(t, 3)
+            scores(t, 2, [lk[1][0], both(lk[1][1], df[0]), both(lambda: round_a(2), df[1]), p01[0], both(p01[1], ky[0], df[2]),
+                          both(lambda: round_a(3), ky[1], df[3])] + p01[2:])
+            run([tr[2], tr[3], ky[2], ch[1][0], ch[1][1], ky[3], ch[1][2], ch[1][3], lk[2][0], lk[3][0], lk[2][1], lk[3][1]])
+            for i in range(4):
+                plain_b(i)
+            run(pick(t, 2, 4) if CFG["g0"] else [p2[0], p3[0], p2[1], p3[1]] + p2[2:] + p3[2:])
+        list_b(t)
+        tail(t)
+
+    fgather("v", RO, 0, 4)
+    fgather("s", RO, 4, 8)
+    for k in range(4):
+        zgather("v", 2 * k, 2 * k + 1)
+        zgather("s", 2 * k + 1, 2 * k + 2)
+        conv_a(k)
+    for k in range(4):
+        round_a(k)
+        turn_a(RO, k)
+    dmas("y", "d_out", [(T.yo[:], T["Ta%d" % RO][:])], ta_keys(RO, 0, 4), ["yo"])
+    for sem, cnt in total.items():
+        g.wait_ge(T.sem[sem], cnt)

@@ -2,7 +2,6 @@ from concourse.mybir import dt, AluOpType, AxisListType, ActivationFunctionType
 
 RO = 8
 EPS = 2.0 ** -14
-CFG = {"side": 0, "g0": 2, "g1": 0, "g2": 3}
 
 
 def _ta_shape(t):
@@ -30,11 +29,14 @@ SCRATCH = {
     "xb": ("sbuf", [128, 4096], "bfloat16"),
     "mx0": ("sbuf", [128, 128, 4, 4], "bfloat16"),
     "mx1": ("sbuf", [128, 128, 4, 4], "bfloat16"),
-    "zb": ("sbuf", [128, 1024], "bfloat16"),
     "oi": ("sbuf", [128, 256], "int32"),
     "LA": ("sbuf", [128, 256], "uint16"),
     "XT": ("sbuf", [128, 2, 2, 128], "bfloat16"),
     "X1": ("sbuf", [128, 2, 128], "bfloat16"),
+    "CW": ("sbuf", [128, 4096], "float32"),
+    "Tf": ("sbuf", [128, 16, 16], "float32"),
+    "xif": ("sbuf", [128, 16, 16], "bfloat16"),
+    "I1": ("sbuf", [128, 128], "float32"),
     "CT": ("sbuf", [128, 2, 128], "float32"),
     "cn": ("sbuf", [128, 128], "float32"),
     "Tb": ("sbuf", [128, 2, 2, 128], "float32"),
@@ -82,7 +84,7 @@ SCRATCH["Lm1"] = ("sbuf", [128, 4, 2, 32], "uint16")
 for _t in range(2, 7):
     SCRATCH["Lm%d" % _t] = ("sbuf", _ta_shape(_t), "uint16")
 
-SEMAPHORES = ["v", "s", "p", "gc", "ls", "d_o", "d_x", "d_xt", "d_c", "d_cb", "d_ex", "d_rl", "d_out", "d_cast"]
+SEMAPHORES = ["v", "s", "p", "gc", "d_ls", "d_o", "d_x", "d_xt", "d_c", "d_cb", "d_ex", "d_rl", "d_out", "d_cast", "d_cl"]
 SEMAPHORES += ["d_ca%d" % _k for _k in range(4)]
 SEMAPHORES += ["m%d_%d" % (_t, _k) for _t in range(RO) for _k in range(4)]
 SEMAPHORES += ["n%d_%d" % (_t, _k) for _t in range(RO) for _k in range(2)]
@@ -96,12 +98,6 @@ def rank_program(g, core, T, topo):
     AF = ActivationFunctionType
     V, S, P = g.vector, g.scalar, g.tensor
     n = len(T.cores)
-    dst = T.cores[(rank + 1) % n]
-    src = T.cores[(rank - 1) % n]
-    rid, pid, _se = topo.addr(dst)
-    mask = topo.mask(core, dst)
-    n_out = len(topo.engines(core, dst))
-    n_in = len(topo.engines(src, core))
 
     queues = {"v": V, "s": S, "p": P, "y": g.sync, "g": g}
     total = {}
@@ -153,13 +149,16 @@ def rank_program(g, core, T, topo):
             total[sem] = total.get(sem, 0) + 16
         done((sem, total[sem]), reads, writes)
 
-    def send(sem, o_, i_, reads, landed):
+    def send(sem, o_, i_, reads, landed, left="d_ls"):
+        dst, src = T.cores[(rank + 1) % n], T.cores[(rank - 1) % n]
+        rid, pid, _se = topo.addr(dst)
         need("g", reads, [])
-        g.remote_dma(o_, i_, T.sem[sem], T.sem.ls, pid, rid, mask)
-        total["ls"] = total.get("ls", 0) + n_out
-        total[sem] = n_in
+        g.remote_dma(o_, i_, T.sem[sem], T.sem[left], pid, rid, topo.mask(core, dst))
+        total[left] = total.get(left, 0) + len(topo.engines(core, dst))
+        done((left, total[left]), reads, [])
+        total[sem] = len(topo.engines(src, core))
         for k in landed:
-            writer[k] = (sem, n_in)
+            writer[k] = (sem, total[sem])
 
     def pcs(name, a=0, b=8):
         return [(name, k) for k in range(a, b)]
@@ -233,8 +232,10 @@ def rank_program(g, core, T, topo):
         op("p", lambda: P.matmul(T.pB[:, w, :, h, :], T.I14[:], T.Tb[:, w, h], True, False), ["I14", "Tb"], ["pB"])
         op("p", lambda: P.matmul(T.pB[:, w, :, h, :], T.nI[:], T.xib[:, w, h], False, True), ["nI", "xib"], ["pB"])
 
-    def list_b(t):
+    def turn_b():
         op("v", lambda: V.transpose(T.Tt[:], T.pB[:]), ["pB"], ["Tt"])
+
+    def list_b(t):
         for r in range(8):
             copy("v", T["BS%d" % t][:, :, :, r], T.Tt[:, :, r, :], ["Tt"], [("BS", t, r)])
         keys = [("BS", t, r) for r in range(8)]
@@ -286,11 +287,6 @@ def rank_program(g, core, T, topo):
     def list_a(t):
         buf = T["Ta%d" % t]
         keys = ta_keys(t, 0, 4)
-        if t == 0:
-            return
-        if t == RO - 1:
-            copy("v", T.LA[:], buf[:], keys, ["LA"])
-            return
         lm = T["Lm%d" % t]
         if t == 1:
             parts = [(lm[:, :, r, :], buf[:, :, :, r]) for r in range(2)]
@@ -300,6 +296,17 @@ def rank_program(g, core, T, topo):
             copy("v", o_, i_, keys, [("Lm", t, i)])
         dmas("y", "d_rl", [(T.LA[:], lm[:])], [("Lm", t, i) for i in range(len(parts))], ["LA"])
 
+    def conv_last(k):
+        dmas("y", "d_cl", [(T.Tf[:, m], T.Z[1::16, 256 * m:256 * m + 256]) for m in range(4 * k, 4 * k + 4)],
+             pcs("Z", 2 * k, 2 * k + 2), [("Tf", k)])
+
+    def list_last():
+        keys = [("Tf", k) for k in range(4)]
+        copy("s", T.xif[:], T.Tf[:], keys, ["xif"])
+        for m in range(16):
+            op("p", lambda: P.matmul(T.pE[:, 4:8, :, :, m], T.I14[:], T.Tf[:, m], True, False), ["I14"] + keys, ["pE"])
+            op("p", lambda: P.matmul(T.pE[:, 4:8, :, :, m], T.nI[:], T.xif[:, m], False, True), ["nI", "xif"], ["pE"])
+
     def stage(q, t, k):
         bank = "pA%d" % (k % 2)
         z0 = 1024 * k
@@ -307,6 +314,10 @@ def rank_program(g, core, T, topo):
         need(q, [], [bank])
         if t >= 2:
             copy(q, T[bank][:], T.Z[:, z0:z0 + 512], rd[:1], [bank])
+        elif q == "p":
+            for j in range(4):
+                op("p", lambda: P.matmul(T[bank][:, 128 * j:128 * j + 128], T.I1[:], T.Z[:, z0 + j:z0 + 1024:8], True, True),
+                   rd + ["I1"], [bank])
         elif t == 0:
             for j in range(4):
                 copy(q, T[bank][:, 128 * j:128 * j + 128], T.Z[:, z0 + j:z0 + 1024:8], rd, [(bank, j)] if j < 3 else [bank])
@@ -361,36 +372,6 @@ def rank_program(g, core, T, topo):
                 op("p", lambda: P.matmul(T[kb][:, 0:256], T.sel[:, c0:c0 + 128], mx[:, 32 * j:32 * j + 32, o::2, :],
                                          False, j == 3 and o == 1), keys, [kb])
 
-    def side_scores(t, k):
-        kb = "pK%d" % (k % 2)
-        mname = "mx%d" % (k % 2)
-        mx = T[mname]
-        wd = 128 if t >= 2 else 256
-
-        def diff(j):
-            if j == 0:
-                copy("s", T.zb[:], T.Z[:, 1024 * k:1024 * k + 1024], pcs("Z", 2 * k, 2 * k + 2), ["zb"])
-            bank = "pA%d" % (k % 2) if j % 2 == 0 else "pB"
-            col = (lambda c, st: T[bank][:, c:512:st]) if j % 2 == 0 else (lambda c, st: T.pB[:, :, :, :, c::st])
-            for s in range(4):
-                jj = (j + s) % 4
-                if t >= 2:
-                    parts = [(col(s, 4), T.zb[:, j:512:4], T.zb[:, 512 + jj:1024:4])]
-                else:
-                    parts = [(col(4 * o + s, 8), T.zb[:, 4 * o + j:1024:16], T.zb[:, 8 + 4 * o + jj:1024:16]) for o in range(2)]
-                for o_, u_, w_ in parts:
-                    op("p", lambda: P.matmul(o_, T.pI[:], u_, True, False), ["pI", "zb"], [bank])
-                    op("p", lambda: P.matmul(o_, T.nI[:], w_, False, True), ["nI", "zb"], [bank])
-            op("s", lambda: S.activation(mx[:, 32 * j:32 * j + 32], T[bank][:], AF.Relu, scale=EPS), [bank],
-               [(mname, j, s) for s in range(4)] + [(mname, j, s, 0) for s in range(4)])
-
-        def keys(j):
-            if j == 0:
-                op("p", lambda: P.matmul(T[kb][:, 0:wd], T.tie[:], T.srow[:, 0:wd], True, False), ["tie", "srow"], [kb])
-            sums(t, k, j)
-
-        return [lambda j=j: diff(j) for j in range(4)], [lambda j=j: keys(j) for j in range(4)]
-
     def least(t, k):
         u = k % 2
         kb = "pK%d" % u
@@ -408,7 +389,6 @@ def rank_program(g, core, T, topo):
         wd = 128 if t >= 2 else 256
         c0, c1 = wd * k0, wd * k1
         p0 = wd * (k0 % 2)
-        ms = T["MS%d" % t]
         ks = lambda name: [(name, k) for k in range(k0, k1)]
         steps = [
             lambda: op("v", lambda: V.tensor_tensor(T.D[:, c0:c1], T[pb][:, p0:p0 + c1 - c0], T.E[:, c0:c1], A.subtract),
@@ -424,6 +404,7 @@ def rank_program(g, core, T, topo):
                ks("SL"), ks("UP1"))
 
         def out():
+            ms = T["MS%d" % t]
             if t >= 2:
                 for b in range(2):
                     copy("v", ms[:, k0:k1, :, b, :], T.UP[:, b, 32 * k0:32 * k1], ks("UP%d" % b), [("MS", t, k0, b)])
@@ -442,9 +423,17 @@ def rank_program(g, core, T, topo):
             f()
 
     def ygather(q, t, a, b):
-        gather(q, "Y", "U", ["U"], "LM%d" % t, 0, [("LM", t, k) for k in range(a // 2, (b + 1) // 2)], a, b, 128.0)
+        keys = [("LM", t, k) for k in range(a // 2, (b + 1) // 2)]
+        if t < RO - 1:
+            gather(q, "Y", "U", ["U"], "LM%d" % t, 0, keys, a, b, 128.0)
+        else:
+            gather(q, "Y", "CW", pcs("CW"), "LM%d" % t, 0, keys, a, b)
 
-    def zgather(q, a, b):
+    def places(k):
+        op("g", lambda: g.iota(T.CW[:, 512 * k:512 * k + 512], [[1, 512]], 512 * k, 0, allow_small_or_imprecise_dtypes=True),
+           [], [("CW", k)])
+
+    def zgather(q, t, a, b):
         gather(q, "Z", "F", pcs("F"), "LA", 0, ["LA"], a, b)
 
     def bgather(q, t, a, b):
@@ -452,15 +441,6 @@ def rank_program(g, core, T, topo):
 
     def fgather(q, t, a, b):
         gather(q, "F", "Y", pcs("Y"), "LB%d" % (t - 1), 0, [("LB", t - 1, 0)], a, b)
-
-    def tail(t):
-        list_a(t)
-        ygather("s" if t else "v", t, 0, 2)
-        ygather("s", t, 2, 4)
-        ygather("v", t, 4, 5)
-        ygather("s", t, 5, 6)
-        ygather("v", t, 6, 7)
-        ygather("s", t, 7, 8)
 
     dmas("y", "d_o", [(T.oi[:], T.o[:])], [], ["oi"])
     dmas("y", "d_x", [(T.xb[:, 0:2048], T.x[:, 0:2048])], [], ["xb"])
@@ -475,6 +455,7 @@ def rank_program(g, core, T, topo):
     op("v", lambda: V.memset(T.e14[:], 16384.0), [], ["e14"])
     dmas("y", "d_xt", [(T.XT[:, w, h], T.x[16 * h + 2 * w::32, :]) for w in range(2) for h in range(2)]
          + [(T.X1[:, h], T.x[16 * h + 1::32, :]) for h in range(2)], [], ["XT", "X1"])
+    op("g", lambda: g.affine_select(T.I1[:], T.one[:], [[-1, 128]], A.is_equal, 0.0, 0, 1), ["one"], ["I1"])
     dmas("g", "d_cast", [(T.U[:], T.x[:])], [], ["U"])
     make_pm(0)
     op("g", lambda: g.affine_select(T.I14[:], T.e14[:], [[-1, 128]], A.is_equal, 0.0, 0, 1), ["e14"], ["I14"])
@@ -517,31 +498,38 @@ def rank_program(g, core, T, topo):
                      round_b(0), put_b(0)),
         ]
 
+    skip = lambda: None
+    both = lambda *fs: (lambda: run(fs))
+    z0 = lambda q, k: gather(q, "Z", "xb", ["xb", "xb2"], "LA", 0, ["LA"], 2 * k, 2 * k + 2, 128.0)
+    conv_b([0])
+    z0("v", 0)
+    stage("p", 0, 0)
+    z0("v", 1)
     fill = []
     for k in range(4):
-        gather("v", "Z", "xb", ["xb", "xb2"], "LA", 0, ["LA"], 2 * k, 2 * k + 2, 128.0)
-        stage("v", 0, k)
-        if k == 1:
+        if k == 2:
             late_setup()
-            conv_b([0])
-        if k == 3:
-            fb = first_b()
-            fill = fill[:2] + [lambda: run(fb[:2]), lambda: run(fb[2:])] + fill[2:]
+        if k < 3:
+            stage("p", 0, k + 1)
         scores(0, k, fill)
+        if k < 2:
+            z0("v", k + 2)
         if k % 2 == 0:
             choices(0, k // 2, range(4))
         fill = least(0, k) + pick(0, k, k + 1)
+    run(first_b())
     for i in range(4):
         plain_b(i)
     run(fill)
+    turn_b()
     list_b(0)
     make_pm(1)
     make_rot()
-    tail(0)
+    ygather("v", 0, 0, 4)
+    ygather("s", 0, 4, 8)
 
-    skip = lambda: None
-    both = lambda *fs: (lambda: run(fs))
     for t in range(1, RO):
+        last = t == RO - 1
         bgather("v", t, 0, 4)
         bgather("s", t, 4, 8)
         conv_b([0, 1])
@@ -551,69 +539,59 @@ def rank_program(g, core, T, topo):
         tr = [lambda k=k: turn_a(t, k) for k in range(4)]
         ch = [[lambda u=u, s=s: choices(t, u, [s]) for s in range(4)] for u in range(2)]
         p01, p2, p3 = pick(t, 0, 2), pick(t, 2, 3), pick(t, 3, 4)
-        zgather("v", 0, 1)
-        zgather("s", 2, 3)
+        pl = [lambda i=i: plain_b(i) for i in range(4)]
+        zgather("v", t, 0, 1)
+        zgather("s", t, 2, 3)
         if t < 2:
-            zgather("v", 1, 2)
+            zgather("v", t, 1, 2)
         stage("s", t, 0)
         if t >= 2:
-            zgather("v", 1, 2)
+            zgather("v", t, 1, 2)
         conv_a(0)
-        zgather("s", 3, 4)
+        zgather("s", t, 3, 4)
         conv_a(1)
-        if not CFG["side"]:
-            round_b(t)
-            scores(t, 0, [])
-            stage("s", t, 1)
-            zgather("s", 4, 6)
-            conv_a(2)
-            put_b(t)
-            round_a(0)
-            scores(t, 1, [skip] * CFG["g2"] + lk[0] + [tr[0]])
-            round_a(1)
-            stage("s", t, 2)
-            zgather("s", 6, 8)
-            conv_a(3)
-            scores(t, 2, [both(tr[1], ch[0][0], ch[0][1]), lk[1][0], both(lk[1][1], ch[0][2], ch[0][3])] + [skip] * CFG["g0"] + p01)
-            stage("s", t, 3)
-            round_a(2)
-            scores(t, 3, [tr[2], lk[2][0], lk[2][1]] + [skip] * CFG["g1"]
-                   + [both(lambda: round_a(3), tr[3], ch[1][0], ch[1][1]), skip, both(ch[1][2], ch[1][3])])
-            for i in range(4):
-                plain_b(i)
-            run([p2[0], lk[3][0], p2[1], lk[3][1]] + p2[2:3] + [p3[0]] + p2[3:] + p3[1:])
-        else:
-            stage("s", t, 1)
-            scores(t, 0, [])
-            round_b(t)
-            zgather("s", 4, 6)
-            conv_a(2)
-            round_a(0)
-            round_a(1)
-            put_b(t)
-            zgather("s", 6, 8)
-            conv_a(3)
-            scores(t, 1, [skip] * CFG["g2"] + lk[0] + [tr[0], both(tr[1], ch[0][0], ch[0][1]), skip, both(ch[0][2], ch[0][3])])
-            stage("s", t, 2)
-            df, ky = side_scores(t, 3)
-            scores(t, 2, [lk[1][0], both(lk[1][1], df[0]), both(lambda: round_a(2), df[1]), p01[0], both(p01[1], ky[0], df[2]),
-                          both(lambda: round_a(3), ky[1], df[3])] + p01[2:])
-            run([tr[2], tr[3], ky[2], ch[1][0], ch[1][1], ky[3], ch[1][2], ch[1][3], lk[2][0], lk[3][0], lk[2][1], lk[3][1]])
-            for i in range(4):
-                plain_b(i)
-            run(pick(t, 2, 4) if CFG["g0"] else [p2[0], p3[0], p2[1], p3[1]] + p2[2:] + p3[2:])
+        round_b(t)
+        scores(t, 0, [])
+        stage("s", t, 1)
+        zgather("s", t, 4, 6)
+        conv_a(2)
+        round_a(0)
+        zgather("s", t, 6, 7)
+        round_a(1)
+        scores(t, 1, [skip] * 3 + lk[0] + [tr[0], both(tr[1], ch[0][0], ch[0][1])])
+        stage("s", t, 2)
+        zgather("s", t, 7, 8)
+        conv_a(3)
+        if last:
+            for k in range(4):
+                conv_last(k)
+        put_b(t)
+        scores(t, 2, [both(ch[0][2], ch[0][3]), lk[1][0], both(lk[1][1], pl[0]), pl[1]]
+               + [both(p01[0], pl[2]), both(p01[1], pl[3])] + p01[2:])
+        stage("s", t, 3)
+        round_a(2)
+        round_a(3)
+        scores(t, 3, [lk[2][0], lk[2][1], both(tr[2], tr[3], ch[1][0], ch[1][1]), skip, both(ch[1][2], ch[1][3])])
+        ygather("s", t, 0, 4)
+        if last:
+            list_last()
+        run([p2[0], turn_b, p2[1], lk[3][0]] + p2[2:3] + [lk[3][1]] + p2[3:] + p3)
         list_b(t)
-        tail(t)
+        if not last:
+            list_a(t)
+        if t <= 4:
+            places(2 * t - 2)
+            places(2 * t - 1)
+        ygather("v", t, 4, 5)
+        ygather("s", t, 5, 6)
+        ygather("v", t, 6, 7)
+        ygather("s", t, 7, 8)
 
     fgather("v", RO, 0, 4)
+    copy("v", T.LA[:], T.pE[:, 4:8], ["pE"], ["LA"])
     fgather("s", RO, 4, 8)
-    for k in range(4):
-        zgather("v", 2 * k, 2 * k + 1)
-        zgather("s", 2 * k + 1, 2 * k + 2)
-        conv_a(k)
-    for k in range(4):
-        round_a(k)
-        turn_a(RO, k)
-    dmas("y", "d_out", [(T.yo[:], T["Ta%d" % RO][:])], ta_keys(RO, 0, 4), ["yo"])
+    zgather("v", RO, 0, 4)
+    zgather("s", RO, 4, 8)
+    dmas("y", "d_out", [(T.yo[:], T.Z[0::16, :])], pcs("Z"), [])
     for sem, cnt in total.items():
         g.wait_ge(T.sem[sem], cnt)

@@ -1,93 +1,78 @@
 from concourse.mybir import dt, AluOpType, AxisListType, ActivationFunctionType
 
 RO = 8
-EPS = 2.0 ** -14
-
-
-def _ta_shape(t):
-    if t == 1:
-        return [128, 4, 32, 2]
-    if 2 <= t <= 6:
-        tb = t - 2
-        return [128, 4, 2, 2 ** (4 - tb), 2, 2 ** tb]
-    return [128, 4, 2, 32]
-
-
-def _msg_shape(t):
-    if t < 2:
-        return [128, 4, 64]
-    tb = t - 2
-    return [128, 4, 2 ** (5 - tb), 2, 2 ** tb]
-
+POS = [0, 1, 2, 3, 4, 7, 8, 9]
+BIG = 2.0 ** 40
 
 SCRATCH = {
-    "U": ("sbuf", [128, 4096], "float32"),
-    "Y": ("sbuf", [128, 4096], "float32"),
-    "F": ("sbuf", [128, 4096], "float32"),
-    "B": ("sbuf", [128, 4096], "float32"),
-    "Z": ("sbuf", [128, 4096], "float32"),
-    "xb": ("sbuf", [128, 4096], "bfloat16"),
-    "mx0": ("sbuf", [128, 128, 4, 4], "bfloat16"),
-    "mx1": ("sbuf", [128, 128, 4, 4], "bfloat16"),
-    "oi": ("sbuf", [128, 256], "int32"),
-    "LA": ("sbuf", [128, 256], "uint16"),
-    "XT": ("sbuf", [128, 2, 2, 128], "bfloat16"),
-    "X1": ("sbuf", [128, 2, 128], "bfloat16"),
+    "X0": ("sbuf", [128, 5120], "float32"),
+    "X1": ("sbuf", [128, 5120], "float32"),
+    "W": ("sbuf", [128, 5120], "float32"),
+    "AO": ("sbuf", [128, 4096], "float32"),
     "CW": ("sbuf", [128, 4096], "float32"),
-    "Tf": ("sbuf", [128, 16, 16], "float32"),
-    "xif": ("sbuf", [128, 16, 16], "bfloat16"),
-    "I1": ("sbuf", [128, 128], "float32"),
-    "CT": ("sbuf", [128, 2, 128], "float32"),
+    "CO": ("sbuf", [128, 4096], "float32"),
+    "CD": ("sbuf", [128, 4, 1024], "float32"),
+    "TH": ("sbuf", [128, 1024], "float32"),
+    "xb": ("sbuf", [128, 4096], "bfloat16"),
+    "UL": ("sbuf", [128, 4, 1152], "bfloat16"),
+    "ML": ("sbuf", [128, 2, 1152, 4], "bfloat16"),
+    "UH": ("sbuf", [128, 8, 640], "bfloat16"),
+    "MH": ("sbuf", [128, 4, 640], "bfloat16"),
+    "oi": ("sbuf", [128, 256], "int32"),
+    "LN": ("sbuf", [128, 256], "uint16"),
+    "LA": ("sbuf", [128, 256], "uint16"),
+    "LR": ("sbuf", [128, 256], "uint16"),
+    "LC": ("sbuf", [128, 256], "uint16"),
+    "LG": ("sbuf", [128, 256], "uint16"),
+    "LS": ("sbuf", [128, 64], "uint16"),
+    "OF": ("sbuf", [128, 8, 4, 2, 4], "float32"),
+    "ED": ("sbuf", [128, 256], "float32"),
+    "EH": ("sbuf", [128, 256], "bfloat16"),
+    "EC": ("sbuf", [128, 256], "float32"),
+    "DD": ("sbuf", [128, 256], "float32"),
+    "DG": ("sbuf", [128, 256], "float32"),
+    "DC": ("sbuf", [128, 256], "float32"),
+    "BD": ("sbuf", [128, 256], "float32"),
+    "BR": ("sbuf", [128, 256], "float32"),
+    "YR": ("sbuf", [128, 256], "float32"),
     "cn": ("sbuf", [128, 128], "float32"),
-    "Tb": ("sbuf", [128, 2, 2, 128], "float32"),
-    "xib": ("sbuf", [128, 2, 2, 128], "bfloat16"),
-    "Tt": ("sbuf", [128, 2, 8, 32], "float32"),
-    "UT": ("sbuf", [128, 2, 2, 128], "float32"),
-    "Tc": ("sbuf", [128, 4, 2, 32], "float32"),
-    "xia": ("sbuf", [128, 4, 2, 32], "bfloat16"),
-    "sel": ("sbuf", [128, 3 * 144], "bfloat16"),
-    "tie": ("sbuf", [128, 128], "bfloat16"),
-    "srow": ("sbuf", [128, 256], "bfloat16"),
-    "rst": ("sbuf", [128, 256], "float32"),
     "one": ("sbuf", [128, 128], "float32"),
-    "big": ("sbuf", [128, 128], "float32"),
-    "e14": ("sbuf", [128, 128], "float32"),
-    "I14": ("sbuf", [128, 128], "float32"),
-    "nI": ("sbuf", [128, 128], "bfloat16"),
-    "pI": ("sbuf", [128, 128], "bfloat16"),
-    "rot": ("sbuf", [128, 8, 32, 4], "float32"),
-    "pm0": ("sbuf", [128, 4, 16, 2, 4], "float32"),
-    "pm1": ("sbuf", [128, 4, 8, 2, 2, 4], "float32"),
-    "RM0": ("sbuf", [128, 256], "float32"),
-    "RM1": ("sbuf", [128, 256], "float32"),
-    "E": ("sbuf", [128, 1024], "float32"),
-    "D": ("sbuf", [128, 1024], "float32"),
-    "SL": ("sbuf", [128, 1024], "int32"),
-    "UP": ("sbuf", [128, 2, 128], "int32"),
-    "pA0": ("psum", [128, 512], "float32"),
-    "pA1": ("psum", [128, 512], "float32"),
+    "SEL": ("sbuf", [128, 5, 144], "bfloat16"),
+    "KL": ("sbuf", [128, 4, 128], "bfloat16"),
+    "KR": ("sbuf", [128, 128], "bfloat16"),
+    "TL": ("sbuf", [128, 4, 128], "bfloat16"),
+    "TR": ("sbuf", [128, 11, 128], "bfloat16"),
+    "rst": ("sbuf", [128, 2, 128], "float32"),
+    "SL": ("sbuf", [128, 2, 128], "int32"),
+    "SA": ("sbuf", [128, 2, 32], "int32"),
+    "RI": ("sbuf", [128, 2, 2, 2, 8], "int32"),
+    "RB": ("sbuf", [128, 64], "bfloat16"),
+    "idn": ("sbuf", [128, 128], "bfloat16"),
+    "MS": ("sbuf", [128, 128], "bfloat16"),
+    "m16": ("sbuf", [128, 8], "bfloat16"),
+    "S16": ("sbuf", [128, 128], "bfloat16"),
+    "tmp": ("sbuf", [128, 128], "int32"),
+    "pc": ("sbuf", [128, 4], "int32"),
+    "pf": ("sbuf", [128, 4], "float32"),
+    "PA": ("sbuf", [128, 4, 144], "float32"),
+    "PB": ("sbuf", [128, 4, 132], "float32"),
     "pK0": ("psum", [128, 512], "float32"),
     "pK1": ("psum", [128, 512], "float32"),
-    "pP0": ("psum", [128, 512], "float32"),
-    "pP1": ("psum", [128, 512], "float32"),
-    "pE": ("psum", [128, 8, 2, 2, 16], "float32"),
-    "pB": ("psum", [128, 2, 8, 2, 16], "float32"),
+    "pL": ("psum", [128, 8, 64], "float32"),
+    "pR": ("psum", [128, 2, 8, 4, 2, 4], "float32"),
+    "pS": ("psum", [128, 512], "float32"),
 }
-for _t in range(RO + 1):
-    SCRATCH["Ta%d" % _t] = ("sbuf", _ta_shape(_t), "float32")
-for _t in range(RO):
-    SCRATCH["MS%d" % _t] = ("sbuf", _msg_shape(_t), "uint16")
-    SCRATCH["LM%d" % _t] = ("sbuf", [128, 256], "uint16")
-    SCRATCH["BS%d" % _t] = ("sbuf", [128, 2, 32, 8], "uint16")
-    SCRATCH["LB%d" % _t] = ("sbuf", [128, 512], "uint16")
-SCRATCH["Lm1"] = ("sbuf", [128, 4, 2, 32], "uint16")
-for _t in range(2, 7):
-    SCRATCH["Lm%d" % _t] = ("sbuf", _ta_shape(_t), "uint16")
+for _t in range(RO - 1):
+    SCRATCH["DS%d" % (_t % 2)] = ("sbuf", [128, 256], "uint16")
+    SCRATCH["DI%d" % (_t % 2)] = ("sbuf", [128, 256], "float32")
+    SCRATCH["LD%d" % _t] = ("sbuf", [128, 256], "uint16")
+    SCRATCH["IR%d" % _t] = ("sbuf", [128, 256], "float32")
 
-SEMAPHORES = ["v", "s", "p", "gc", "d_ls", "d_o", "d_x", "d_xt", "d_c", "d_cb", "d_ex", "d_rl", "d_out", "d_cast", "d_cl"]
-SEMAPHORES += ["d_ca%d" % _k for _k in range(4)]
+SEMAPHORES = ["v", "s", "p", "gc", "d_ls", "d_l2", "d_o", "d_x", "d_z", "d_q1", "d_q2", "d_g0", "d_j", "d_b", "d_cw", "d_ex", "d_cd",
+              "d_w", "d_ac", "d_i", "d_out", "ra", "rb"]
+SEMAPHORES += ["d_%s%d" % (_n, _k) for _n in "dc" for _k in range(4)]
 SEMAPHORES += ["m%d_%d" % (_t, _k) for _t in range(RO) for _k in range(4)]
-SEMAPHORES += ["n%d_%d" % (_t, _k) for _t in range(RO) for _k in range(2)]
+SEMAPHORES += ["n%d" % _t for _t in range(RO - 1)]
 
 
 def rank_program(g, core, T, topo):
@@ -142,15 +127,15 @@ def rank_program(g, core, T, topo):
         total[sem] = total.get(sem, 0) + 1
         done((sem, total[sem]), reads, writes)
 
-    def dmas(q, sem, pairs, reads, writes):
+    def dmas(q, sem, pairs, reads, writes, **kw):
         need(q, reads, writes)
         for o_, i_ in pairs:
-            queues[q].dma_start(o_, i_).then_inc(T.sem[sem], 16)
+            queues[q].dma_start(o_, i_, **kw).then_inc(T.sem[sem], 16)
             total[sem] = total.get(sem, 0) + 16
         done((sem, total[sem]), reads, writes)
 
-    def send(sem, o_, i_, reads, landed, left="d_ls"):
-        dst, src = T.cores[(rank + 1) % n], T.cores[(rank - 1) % n]
+    def send(sem, o_, i_, reads, landed, hop=1, left="d_ls"):
+        dst, src = T.cores[(rank + hop) % n], T.cores[(rank - hop) % n]
         rid, pid, _se = topo.addr(dst)
         need("g", reads, [])
         g.remote_dma(o_, i_, T.sem[sem], T.sem[left], pid, rid, topo.mask(core, dst))
@@ -163,435 +148,383 @@ def rank_program(g, core, T, topo):
     def pcs(name, a=0, b=8):
         return [(name, k) for k in range(a, b)]
 
-    def gather(q, out, win, wkeys, lst, off, lkeys, a, b, add=None):
-        if a >= b:
+    def gather(q, o_, win, lst, reads, writes, scale=None, add=None):
+        i_ = win.indirect(lst)
+        if q == "s":
+            fn = lambda: S.activation(o_, i_, AF.Identity, bias=(add or 0.0), scale=(scale or 1.0))
+        elif scale is not None:
+            fn = lambda: V.tensor_scalar(o_, i_, scale, None, A.mult)
+        elif add is not None:
+            fn = lambda: V.tensor_scalar(o_, i_, add, None, A.add)
+        else:
+            fn = lambda: V.tensor_copy(o_, i_)
+        op(q, fn, reads, writes)
+
+    def copy(o_, i_, reads, writes):
+        op("v", lambda: V.tensor_copy(o_, i_), reads, writes)
+
+    def fill(ap, val, key):
+        op("v", lambda: V.memset(ap, val), [], [key])
+
+    def iota(ap, pattern, base, cm, reads, writes):
+        op("g", lambda: g.iota(ap, pattern, base, cm, allow_small_or_imprecise_dtypes=True), reads, writes)
+
+    def mm(o_, l_, r_, start, stop, reads, bank):
+        op("p", lambda: P.matmul(o_, l_, r_, start, stop), reads, [bank])
+
+    def xname(t):
+        return "X%d" % (t % 2)
+
+    def a_piece(q, k):
+        gather(q, T.AO[:, 512 * k:512 * k + 512], T.W[:, 0:4096], T.LC[:, 32 * k:32 * k + 32], ["W", ("LC", k // 2)], [("AO", k)])
+
+    def b_piece(q, t, k):
+        x, y = xname(t), xname(t + 1)
+        gather(q, T[y][:, 512 * k:512 * k + 512], T[x][:, 0:4096], T["LD%d" % t][:, 32 * k:32 * k + 32],
+               pcs(x) + [("LD", t, k // 2)], [(y, k)])
+
+    def c_piece(q, lst, k, u, add=None):
+        c0 = 64 * k + 16 * u
+        gather(q, T.CO[:, 1024 * k + u:1024 * k + 1024:4], T.CW[:], T[lst][:, c0:c0 + 16], ["CW", (lst, k)], [("CO", k, u)], add=add)
+
+    def c_dense(k):
+        dmas("y", "d_c%d" % k, [(T.DC[:, 64 * k:64 * k + 64], T.CO[0::16, 1024 * k:1024 * k + 1024])],
+             [("CO", k, u) for u in range(4)], [("DC", k)])
+
+    def c_list(k):
+        copy(T.LC[:, 64 * k:64 * k + 64], T.DC[:, 64 * k:64 * k + 64], [("DC", k)], [("LC", k)])
+
+    def a_dense(name, sem, row, k0, k1):
+        dmas("y", sem, [(T[name][:, 64 * k:64 * k + 64], T.AO[row::16, 1024 * k:1024 * k + 1024]) for k in range(k0, k1)],
+             pcs("AO", 2 * k0, 2 * k1), [(name, k) for k in range(k0, k1)] + ["zero"] * (name == "DD" and k0 == 0))
+
+    def d_send(t, k):
+        ds = "DS%d" % (t % 2)
+        cols = slice(64 * k, 64 * k + 64)
+        if t == RO - 1:
+            send("m%d_%d" % (t, k), T.YR[:, cols], T.DD[:, cols], [("DD", k)], [("YR", k)])
             return
-        o_ = T[out][:, 512 * a:512 * b]
-        i_ = T[win][:, 0:4096].indirect(T[lst][:, off + 32 * a:off + 32 * b])
+        copy(T[ds][:, cols], T.DD[:, cols], [("DD", k)], [(ds, k)])
+        send("m%d_%d" % (t, k), T["LD%d" % t][:, cols], T[ds][:, cols], [(ds, k)], [("LD", t, k)])
+
+    def extract(name, row, dst):
+        dmas("y", "d_ex", [(T[dst][j::4, :], T[name][row::16, 1024 * j:1024 * j + 1024]) for j in range(4)], pcs(name), [dst])
+
+    def strip_s():
+        op("s", lambda: S.activation(T.EH[:], T.ED[:], AF.Identity, bias=128.0, scale=2.0 ** -14), ["ED"], ["EH"])
+        op("s", lambda: S.activation(T.pS[:, 0:256], T.EH[:], AF.Identity, bias=2.0 ** 21, scale=-16384.0), ["EH"], ["pS"])
+
+    def strip_v():
+        op("v", lambda: V.tensor_tensor(T.EC[:], T.ED[:], T.pS[:, 0:256], A.add), ["ED", "pS"], ["EC"])
+
+    def turned(row):
+        dmas("y", "d_cd", [(T.CD[4 * j + row::16, :, 256 * r:256 * r + 256], T.EC[(j + r) % 4::4, :])
+                           for r in range(4) for j in range(4)], ["EC"], ["CD"])
+
+    def select(q, t, u):
+        far = u ^ (2 ** (POS[t] - 8)) if POS[t] >= 8 else u
+        gather(q, T.TH[:, 256 * u:256 * u + 256], T.CD[:, far, :], T.LS[:, 16 * u:16 * u + 16], ["CD", "CDj", "LS0", "LS1"], [("TH", u)])
+
+    def spread(t):
+        th = pcs("TH", 0, 4)
+        pairs = [(T.W[0::16, 0:4096], T.TH[0::4, :])]
+        if t < RO - 1:
+            pairs += [(T.W[2::16, 0:4096], T.TH[1::4, :]), (T.W[1::16, 1024:5120], T.TH[0::4, :]), (T.W[1::16, 0:1024], T.TH[12::16, :])]
+        dmas("y", "d_w", pairs, th, ["W"] + pcs("W"))
+        if t < RO - 2:
+            x = xname(t)
+            dmas("g", "d_ac", [(T[x][t::16, 1024:5120], T.TH[0::4, :]), (T[x][t::16, 0:1024], T.TH[12::16, :])],
+                 th + [(x, "j")], pcs(x), accum_op=A.add, max_dma_last_dim=4096)
+
+    def narrow(q, o_, i_, m, reads, writes):
         if q == "v":
-            if add is None:
-                fn = lambda: V.tensor_copy(o_, i_)
-            else:
-                fn = lambda: V.tensor_scalar(o_, i_, add, None, A.add)
+            op(q, lambda: V.tensor_scalar(o_, i_, 2.0 ** -14, 128.0 + 16 * m, A.mult, A.add), reads, writes)
         else:
-            fn = lambda: S.activation(o_, i_, AF.Identity, bias=(add or 0.0))
-        op(q, fn, wkeys + lkeys, pcs(out, a, b))
+            op(q, lambda: S.activation(o_, i_, AF.Identity, bias=128.0 + 16 * m, scale=2.0 ** -14), reads, writes)
 
-    def copy(q, o_, i_, reads, writes):
-        if q == "v":
-            op(q, lambda: V.tensor_copy(o_, i_), reads, writes)
-        else:
-            op(q, lambda: S.activation(o_, i_, AF.Identity), reads, writes)
+    def low_bits(p, b, m, h):
+        if p == 4:
+            return 16 * b + 8 * h + m
+        return 16 * h + ((m >> p) << (p + 1)) + (b << p) + (m & (2 ** p - 1))
 
-    def pieces(d):
-        d %= 4
-        return [(0, 4 - d, d)] + ([(4 - d, d, 0)] if d else [])
+    def narrow_low(q, t, h, b, ms):
+        x = xname(t)
+        for m in ms:
+            narrow(q, T.UL[:, 2 * h + b, m::9], T[x][:, low_bits(POS[t], b, m, h):4096:32], m, pcs(x) + ["UL"], [("UL", h, b, m)])
 
-    def make_rot():
-        for h, ones in ((0, "one"), (1, "big")):
-            for d in range(4):
-                for j0, c, w0 in pieces(d):
-                    op("g", lambda: g.affine_select(T.rot[:, 4 * h + d, :, j0:j0 + c], T[ones][:, 0:32 * c], [[-4, 32], [-1, c]],
-                                                    A.is_equal, 0.0, -w0, 1), [ones], [("rot", h, d, j0)])
-
-    def make_pm(t):
+    def scan_low(t, h, j):
+        p = POS[t]
+        bank = "pK%d" % (h if p < 4 else 0)
+        rd = [("UL", h, b, m) for b in range(2) for m in range(8)]
+        if j == 0 and (p < 4 or h == 0):
+            mm(T[bank][:, 0:128], T.KL[:, min(p, 3)], T.KR[:], True, False, [("KL", min(p, 3)), "KR"], bank)
         for s in range(4):
-            for b in range(2):
-                for j0, c, w0 in pieces(s if b == 0 else 1 - s):
-                    if t == 0:
-                        fn = lambda: g.affine_select(T.pm0[:, s, :, b, j0:j0 + c], T.one[:, 0:16 * c], [[-8, 16], [-1, c]],
-                                                     A.is_equal, 0.0, -(4 * (1 - b) + w0), 1)
-                    else:
-                        fn = lambda: g.affine_select(T.pm1[:, s, :, b, :, j0:j0 + c], T.one[:, 0:16 * c],
-                                                     [[-16, 8], [-4, 2], [-1, c]], A.is_equal, 0.0, -(8 * (1 - b) + w0), 1)
-                    op("g", fn, ["one"], [("pm", t, s, b, j0)])
+            jj = (j + s) % 4
+            op("v", lambda: V.tensor_tensor_scan(T.ML[:, h, 288 * j:288 * j + 288, s], T.UL[:, 2 * h, 288 * j:288 * j + 288],
+                                                 T.UL[:, 2 * h + 1, 288 * jj:288 * jj + 288], 0.0, A.max, A.min), rd, [("ML", h, j, s)])
+        for m in range(8):
+            c0 = low_bits(p, 0, m, h) % 16
+            mm(T[bank][:, 0:128], T.SEL[:, p, 16 - c0:144 - c0], T.ML[:, h, 288 * j + m:288 * j + 288:9, :], False, False,
+               [("ML", h, j, s) for s in range(4)] + ["SEL"], bank)
+        if j == 3 and (p < 4 or h == 1):
+            r = 2 * p + h if p < 4 else 8
+            mm(T[bank][:, 0:128], T.TL[:, min(p, 3)], T.TR[:, r], False, True, [("TL", min(p, 3)), ("TR", r), "TL", "TR"], bank)
 
-    def rot_keys(h, d):
-        return [("rot", h, d, j0) for j0, _c, _w in pieces(d)]
+    def least(w, h, bank):
+        op("v", lambda: V.tensor_tensor_scan(T.SL[:, h], T.rst[:, w], T[bank][:, 0:128], 0.0, A.add, A.min), ["rst", bank], [("SL", h)])
 
-    def pm_keys(t, s):
-        return [("pm", t, s, b, j0) for b in range(2) for j0, _c, _w in pieces(s if b == 0 else 1 - s)]
-
-    def conv_b(parts):
-        dmas("y", "d_cb", [(T.Tb[:, w, h], T.B[16 * h + 2 * w::32, :]) for w in parts for h in range(2)], pcs("B"), ["Tb"])
-
-    def round_b(t):
-        copy("s", T.xib[:], T.Tb[:], ["Tb"], ["xib"])
-        if t < RO - 1:
-            op("p", lambda: P.matmul(T.pB[:], T.I14[:], T.Tb[:], True, False), ["I14", "Tb"], ["pB"])
-            op("p", lambda: P.matmul(T.pB[:], T.nI[:], T.xib[:], False, False), ["nI", "xib"], ["pB"])
-            op("p", lambda: P.matmul(T.pB[:], T.pI[:], T.XT[:], False, True), ["pI", "XT"], ["pB"])
-
-    def put_b(t):
-        if t < RO - 1:
-            op("s", lambda: S.activation(T.UT[:], T.pB[:], AF.Identity, scale=EPS), ["pB"], ["UT"])
-            dmas("y", "d_ex", [(T.U[16 * h + 2 * w::32, :], T.UT[:, w, h]) for w in range(2) for h in range(2)], ["UT"], ["U"])
-
-    def plain_b(i):
-        w, h = i // 2, i % 2
-        op("p", lambda: P.matmul(T.pB[:, w, :, h, :], T.I14[:], T.Tb[:, w, h], True, False), ["I14", "Tb"], ["pB"])
-        op("p", lambda: P.matmul(T.pB[:, w, :, h, :], T.nI[:], T.xib[:, w, h], False, True), ["nI", "xib"], ["pB"])
-
-    def turn_b():
-        op("v", lambda: V.transpose(T.Tt[:], T.pB[:]), ["pB"], ["Tt"])
-
-    def list_b(t):
-        for r in range(8):
-            copy("v", T["BS%d" % t][:, :, :, r], T.Tt[:, :, r, :], ["Tt"], [("BS", t, r)])
-        keys = [("BS", t, r) for r in range(8)]
-        if t < RO - 1:
-            send("n%d_1" % t, T["LB%d" % t][:, 256:512], T["BS%d" % t][:, 1], keys, [("LB", t, 1)])
-        send("n%d_0" % t, T["LB%d" % t][:, 0:256], T["BS%d" % t][:, 0], keys, [("LB", t, 0)])
-
-    def conv_a(k):
-        dmas("y", "d_ca%d" % k, [(T.Tc[:, k, h], T.Z[16 * h + 1::32, 1024 * k:1024 * k + 1024]) for h in range(2)],
-             pcs("Z", 2 * k, 2 * k + 2), [("Tc", k)])
-
-    def round_a(k):
-        copy("s", T.xia[:, k], T.Tc[:, k], [("Tc", k)], [("xia", k)])
-        op("p", lambda: P.matmul(T.pE[:, k], T.I14[:], T.Tc[:, k], True, False), ["I14", ("Tc", k)], ["pE"])
-        op("p", lambda: P.matmul(T.pE[:, k], T.nI[:], T.xia[:, k], False, True), ["nI", ("xia", k)], ["pE"])
-
-    def low(t, k, r):
-        buf = T["Ta%d" % t]
-        if t == 1:
-            return buf[:, k, :, r]
-        if t == 2:
-            return buf[:, k, :, :, r, :]
-        if 2 < t <= 6:
-            return buf[:, k, :, :, :, r::2]
-        return buf[:, k, :, r::2]
-
-    def ta_keys(t, k0, k1):
-        return [("Ta", t, k, r) for k in range(k0, k1) for r in range(2)]
-
-    def turn_a(t, k):
-        for r in range(2):
-            op("v", lambda: V.transpose(low(t, k, r), T.pE[:, k, :, r, :]), ["pE"], [("Ta", t, k, r)])
-
-    def choices(t, u, shifts):
-        bank = "pP%d" % u
-        buf = T["Ta%d" % t]
-        k0, k1 = 2 * u, 2 * u + 2
-        for s in shifts:
-            if t < 2:
-                op("p", lambda: P.matmul(T[bank][:, s:512:4], T["pm%d" % t][:, s], buf[:, k0:k1], True, True),
-                   ta_keys(t, k0, k1) + pm_keys(t, s), [bank])
-            else:
-                d = (1 - s) % 4
-                op("p", lambda: P.matmul(T[bank][:, s:256:4], T.rot[:, 4 + s], buf[:, k0:k1, 1], True, False),
-                   ta_keys(t, k0, k1) + rot_keys(1, s), [bank])
-                op("p", lambda: P.matmul(T[bank][:, s:256:4], T.rot[:, d], buf[:, k0:k1, 0], False, True),
-                   ta_keys(t, k0, k1) + rot_keys(0, d), [bank])
-
-    def list_a(t):
-        buf = T["Ta%d" % t]
-        keys = ta_keys(t, 0, 4)
-        lm = T["Lm%d" % t]
-        if t == 1:
-            parts = [(lm[:, :, r, :], buf[:, :, :, r]) for r in range(2)]
+    def offsets_low(t, h):
+        if POS[t] < 4:
+            least(0, h, "pK%d" % h)
+            hs = [h]
         else:
-            parts = [(lm[:, :, y, :, x, :], buf[:, :, x, :, y, :]) for x in range(2) for y in range(2)]
-        for i, (o_, i_) in enumerate(parts):
-            copy("v", o_, i_, keys, [("Lm", t, i)])
-        dmas("y", "d_rl", [(T.LA[:], lm[:])], [("Lm", t, i) for i in range(len(parts))], ["LA"])
+            least(1, 1, "pK0")
+            least(0, 0, "pK0")
+            op("v", lambda: V.tensor_scalar(T.SL[:, 1, 3::4], T.SL[:, 1, 3::4], -272.0, None, A.add), [("SL", 1)], [("SL", 1)])
+            hs = [0, 1]
+        h0, h1 = hs[0], hs[-1] + 1
+        op("v", lambda: V.tensor_scalar(T.SA[:, h0:h1], T.SL[:, h0:h1, 3::4], 1023, None, A.bitwise_and),
+           [("SL", k) for k in hs], [("SA", k) for k in hs])
+        for k in hs:
+            copy(T.LS[:, k::2], T.SA[:, k], [("SA", k)], ["LS%d" % k])
 
-    def conv_last(k):
-        dmas("y", "d_cl", [(T.Tf[:, m], T.Z[1::16, 256 * m:256 * m + 256]) for m in range(4 * k, 4 * k + 4)],
-             pcs("Z", 2 * k, 2 * k + 2), [("Tf", k)])
+    def narrow_high(q, t, b, j):
+        x = xname(t)
+        e = POS[t] - 7
+        for m in range(4):
+            top = ((m >> e) << (e + 1)) + (b << e) + (m & (2 ** e - 1))
+            c0 = 1024 * j + 128 * top
+            narrow(q, T.UH[:, 4 * b + j, m::5], T[x][:, c0:c0 + 128], m, pcs(x, 2 * j, 2 * j + 2) + ["UH"], [("UH", b, j, m)])
 
-    def list_last():
-        keys = [("Tf", k) for k in range(4)]
-        copy("s", T.xif[:], T.Tf[:], keys, ["xif"])
-        for m in range(16):
-            op("p", lambda: P.matmul(T.pE[:, 4:8, :, :, m], T.I14[:], T.Tf[:, m], True, False), ["I14"] + keys, ["pE"])
-            op("p", lambda: P.matmul(T.pE[:, 4:8, :, :, m], T.nI[:], T.xif[:, m], False, True), ["nI", "xif"], ["pE"])
+    def scan_high(i, j, jj):
+        s = (jj - j) % 4
+        if i == 0:
+            mm(T.pK0[:, 0:128], T.idn[:], T.MS[:], True, False, ["idn", "MS"], "pK0")
+        op("v", lambda: V.tensor_tensor_scan(T.MH[:, i % 4], T.UH[:, j], T.UH[:, 4 + jj], 0.0, A.max, A.min),
+           [("UH", b, y, m) for b, y in ((0, j), (1, jj)) for m in range(4)], [("MH", i % 4)])
+        for m in range(4):
+            mm(T.pK0[:, 32 * m + s:32 * m + 32:4], T.MH[:, i % 4, m::5], T.m16[:], False, i == 15 and m == 3, [("MH", i % 4), "m16"], "pK0")
 
-    def stage(q, t, k):
-        bank = "pA%d" % (k % 2)
-        z0 = 1024 * k
-        rd = pcs("Z", 2 * k, 2 * k + 2)
-        need(q, [], [bank])
-        if t >= 2:
-            copy(q, T[bank][:], T.Z[:, z0:z0 + 512], rd[:1], [bank])
-        elif q == "p":
-            for j in range(4):
-                op("p", lambda: P.matmul(T[bank][:, 128 * j:128 * j + 128], T.I1[:], T.Z[:, z0 + j:z0 + 1024:8], True, True),
-                   rd + ["I1"], [bank])
-        elif t == 0:
-            for j in range(4):
-                copy(q, T[bank][:, 128 * j:128 * j + 128], T.Z[:, z0 + j:z0 + 1024:8], rd, [(bank, j)] if j < 3 else [bank])
-        else:
-            for j in range(4):
-                for o in range(2):
-                    copy(q, T[bank][:, 128 * j + o:128 * j + 128:2], T.Z[:, z0 + 4 * o + j:z0 + 1024:16], rd,
-                         [(bank, j, o)] if (j, o) != (3, 1) else [bank])
+    def offsets_high(t):
+        e = POS[t] - 7
+        side = lambda b: [T.RI[:, :, :, b, :], T.RI[:, :, b, :, :], T.RI[:, b, :, :, :]][e]
+        r = 9 if e == 0 else 10
+        mm(T.pL[:, 0], T.TL[:, 0], T.TR[:, r, 0:64], True, False, [("TL", 0), ("TR", r), "TL", "TR"], "pL")
+        least(0, 0, "pK0")
+        op("v", lambda: V.tensor_scalar(side(0), T.SL[:, 0, 3::4], 2, 3, A.logical_shift_right, A.bitwise_and), [("SL", 0)], ["RI0"])
+        op("v", lambda: V.tensor_scalar(side(1), T.SL[:, 0, 3::4], 3, None, A.bitwise_and), [("SL", 0)], ["RI1"])
+        copy(T.RB[:], T.RI[:], ["RI0", "RI1"], ["RB"])
+        mm(T.pL[:, 0], T.S16[:], T.RB[:], False, True, ["S16", "RB"], "pL")
+        copy(T.LS[:], T.pL[:, 0], ["pL"], ["LS0", "LS1"])
 
-    def scores(t, k, fill):
-        bank = "pA%d" % (k % 2)
-        kb = "pK%d" % (k % 2)
-        mname = "mx%d" % (k % 2)
-        mx = T[mname]
-        z0 = 1024 * k
-        rd = pcs("Z", 2 * k, 2 * k + 2) + [bank]
-        wd = 128 if t >= 2 else 256
-        fill = list(fill)
-        op("p", lambda: P.matmul(T[kb][:, 0:wd], T.tie[:], T.srow[:, 0:wd], True, False), ["tie", "srow"], [kb])
-        for j in range(4):
-            for s in range(4):
-                jj = (j + s) % 4
-                if t >= 2:
-                    op("v", lambda: V.tensor_tensor(mx[:, 32 * j:32 * j + 32, :, s], T[bank][:, j:512:4],
-                                                    T.Z[:, z0 + 512 + jj:z0 + 1024:4], A.max), rd, [(mname, j, s)])
-                elif t == 0:
-                    op("v", lambda: V.tensor_tensor(mx[:, 32 * j:32 * j + 32, :, s], T[bank][:, 128 * j:128 * j + 128],
-                                                    T.Z[:, z0 + 4 + jj:z0 + 1024:8], A.max), rd, [(mname, j, s)])
-                else:
-                    for o in range(2):
-                        op("v", lambda: V.tensor_tensor(mx[:, 32 * j:32 * j + 32, o::2, s], T[bank][:, 128 * j + o:128 * j + 128:2],
-                                                        T.Z[:, z0 + 8 + 4 * o + jj:z0 + 1024:16], A.max), rd,
-                           [(mname, j, s)] if o else [(mname, j, s, 0)])
-                if s % 2 == 1 and fill:
-                    fill.pop(0)()
-            sums(t, k, j)
-        for f in fill:
-            f()
+    def const_low(p):
+        iota(T.KL[0:1, p], [[0, 128 // 2 ** p], [16, 2 ** p]], 135, 0, ["KL"], [("KL", p, 0)])
+        iota(T.KL[32:33, p], [[0, 8], [16 * 2 ** p, 8 // 2 ** p], [0, 2 ** (p + 1)]], 0, 0, ["KL", ("KL", p, 0)], [("KL", p)])
+        iota(T.TL[32:33, p], [[0, 64 // 2 ** p], [1, 2], [0, 2 ** p]], 0, 0, ["TL"], [("TL", p)])
+        iota(T.TR[32:33, 2 * p:2 * p + 2], [[0, 128], [-512, 2]], 256 - 2 ** (p + 1), 0, ["TR"], [("TR", p, 0)])
+        for h in range(2):
+            iota(T.TR[64:65, 2 * p + h], [[0, 4], [32, 8], [0, 4]], 16 * h + 2 ** p, 0, ["TR", ("TR", p, 0)], [("TR", 2 * p + h)])
 
-    def sums(t, k, j):
-        kb = "pK%d" % (k % 2)
-        mname = "mx%d" % (k % 2)
-        mx = T[mname]
-        keys = [(mname, j, s) for s in range(4)] + [(mname, j, s, 0) for s in range(4)] + ["sel"]
-        if t >= 2:
-            for o in range(4):
-                op("p", lambda: P.matmul(T[kb][:, 0:128], T.sel[:, 12 - 4 * o:140 - 4 * o], mx[:, 32 * j:32 * j + 32, o, :],
-                                         False, j == 3 and o == 3), keys, [kb])
-        else:
-            for o in range(2):
-                c0 = 144 + 8 - 8 * o if t == 0 else 288 + 4 - 4 * o
-                op("p", lambda: P.matmul(T[kb][:, 0:256], T.sel[:, c0:c0 + 128], mx[:, 32 * j:32 * j + 32, o::2, :],
-                                         False, j == 3 and o == 1), keys, [kb])
+    def const_high():
+        iota(T.TR[64:65, 8], [[0, 4], [32, 8], [0, 4]], 16, 0, ["TR"], [("TR", 8)])
+        iota(T.TR[64:65, 9, 0:64], [[0, 4], [-128, 2], [16, 8]], 128, 0, ["TR"], [("TR", 9)])
+        iota(T.TR[64:65, 10, 0:64], [[0, 4], [128, 2], [16, 8]], 0, 0, ["TR"], [("TR", 10)])
+        op("g", lambda: g.affine_select(T.idn[:], T.one[:], [[-1, 128]], A.is_equal, 0.0, 0, 1), ["one"], ["idn"])
+        iota(T.MS[:], [[0, 32], [10, 2], [3, 2]], 1, 0, [], ["MS"])
+        op("g", lambda: g.affine_select(T.MS[:], T.MS[:], [[0, 4], [-16, 8], [0, 4]], A.is_ge, 0.0, 0, 1), ["MS"], ["MS"])
+        op("g", lambda: g.affine_select(T.MS[:], T.MS[:], [[0, 4], [16, 8], [0, 4]], A.is_ge, 0.0, 15, -1), ["MS"], ["MS"])
+        op("g", lambda: g.iota(T.tmp[:], [[0, 8], [-1, 16]], 16, 1), [], ["tmp"])
+        for y in range(4):
+            op("g", lambda: g.affine_select(T.PB[:, y, 3:131], T.one[:], [[-16, 8], [-1, 4], [-1000, 4]], A.is_equal, 0.0, -4 * y, 1),
+               ["one", "PB"], [("PB", y)])
 
-    def least(t, k):
-        u = k % 2
-        kb = "pK%d" % u
-        wd = 128 if t >= 2 else 256
-        rm = T["RM%d" % u]
-        return [
-            lambda: op("v", lambda: V.tensor_tensor_scan(rm[:, 0:wd], T.rst[:, 0:wd], T[kb][:, 0:wd], 0.0, A.add, A.min),
-                       ["rst", kb], [("RM", u)]),
-            lambda: op("v", lambda: V.tensor_tensor(T.E[:, wd * k:wd * k + wd], T[kb][:, 0:wd], rm[:, 0:wd], A.subtract),
-                       [kb, ("RM", u)], [("E", k)]),
-        ]
-
-    def pick(t, k0, k1):
-        pb = "pP%d" % (k0 // 2)
-        wd = 128 if t >= 2 else 256
-        c0, c1 = wd * k0, wd * k1
-        p0 = wd * (k0 % 2)
-        ks = lambda name: [(name, k) for k in range(k0, k1)]
-        steps = [
-            lambda: op("v", lambda: V.tensor_tensor(T.D[:, c0:c1], T[pb][:, p0:p0 + c1 - c0], T.E[:, c0:c1], A.subtract),
-                       [pb] + ks("E"), ks("D")),
-            lambda: op("v", lambda: V.tensor_tensor_scan(T.SL[:, c0:c1], T.E[:, c0:c1], T.D[:, c0:c1], 0.0, A.min, A.max),
-                       ks("E") + ks("D"), ks("SL")),
-        ]
-
-        def unpack():
-            op("v", lambda: V.tensor_scalar(T.UP[:, 0, 32 * k0:32 * k1], T.SL[:, c0 + 3:c1:4], 12, None, A.logical_shift_right),
-               ks("SL"), ks("UP0"))
-            op("v", lambda: V.tensor_scalar(T.UP[:, 1, 32 * k0:32 * k1], T.SL[:, c0 + 3:c1:4], 4095, None, A.bitwise_and),
-               ks("SL"), ks("UP1"))
-
-        def out():
-            ms = T["MS%d" % t]
-            if t >= 2:
-                for b in range(2):
-                    copy("v", ms[:, k0:k1, :, b, :], T.UP[:, b, 32 * k0:32 * k1], ks("UP%d" % b), [("MS", t, k0, b)])
-            else:
-                copy("v", ms[:, k0:k1], T.SL[:, c0 + 3:c1:4], ks("SL"), [("MS", t, k0, 0)])
-            send("m%d_%d" % (t, k0), T["LM%d" % t][:, 64 * k0:64 * k1], ms[:, k0:k1],
-                 [("MS", t, k0, 0), ("MS", t, k0, 1)], [("LM", t, k) for k in range(k0, k1)])
-
-        if t >= 2:
-            steps.append(unpack)
-        steps.append(out)
-        return steps
-
-    def run(steps):
-        for f in steps:
-            f()
-
-    def ygather(q, t, a, b):
-        keys = [("LM", t, k) for k in range(a // 2, (b + 1) // 2)]
-        if t < RO - 1:
-            gather(q, "Y", "U", ["U"], "LM%d" % t, 0, keys, a, b, 128.0)
-        else:
-            gather(q, "Y", "CW", pcs("CW"), "LM%d" % t, 0, keys, a, b)
-
-    def places(k):
-        op("g", lambda: g.iota(T.CW[:, 512 * k:512 * k + 512], [[1, 512]], 512 * k, 0, allow_small_or_imprecise_dtypes=True),
-           [], [("CW", k)])
-
-    def zgather(q, t, a, b):
-        gather(q, "Z", "F", pcs("F"), "LA", 0, ["LA"], a, b)
-
-    def bgather(q, t, a, b):
-        gather(q, "B", "Y", pcs("Y"), "LB%d" % (t - 1), 256, [("LB", t - 1, 1)], a, b)
-
-    def fgather(q, t, a, b):
-        gather(q, "F", "Y", pcs("Y"), "LB%d" % (t - 1), 0, [("LB", t - 1, 0)], a, b)
+    def const_high_v():
+        op("v", lambda: V.tensor_scalar(T.tmp[:], T.tmp[:], 15, None, A.bitwise_and), ["tmp"], ["tmp"])
+        op("v", lambda: V.tensor_scalar(T.S16[:], T.tmp[:], 0.0, 256.0, A.is_equal, A.mult), ["tmp"], ["S16"])
+        fill(T.m16[:], -16.0, "m16")
+        fill(T.UH[:, :, 4::5], 0.0, "UH")
+        fill(T.PB[:, :, 0:3], 0.0, "PB")
 
     dmas("y", "d_o", [(T.oi[:], T.o[:])], [], ["oi"])
+    fill(T.DD[:], 0.0, "zero")
+    fill(T.one[:], 1.0, "one")
+    fill(T.PA[:, :, 0:12], 0.0, "PA")
+    dmas("y", "d_z", [(T.AO[0::16, :], T.DD[:]), (T.X1[0::16, 0:4096], T.DD[:])], ["zero"], ["AOz", "X1z"])
     dmas("y", "d_x", [(T.xb[:, 0:2048], T.x[:, 0:2048])], [], ["xb"])
     dmas("s", "d_x", [(T.xb[:, 2048:4096], T.x[:, 2048:4096])], [], ["xb2"])
-    copy("v", T.LA[:], T.oi[:], ["oi"], ["LA"])
-    for k in range(4):
-        op("g", lambda: g.iota(T.F[:, 1024 * k:1024 * k + 1024], [[1, 1024]], 128 + 1024 * k, 0, allow_small_or_imprecise_dtypes=True),
-           [], pcs("F", 2 * k, 2 * k + 2))
-        op("s", lambda: S.activation(T.B[:, 0:4096].indirect(T.LA[:, 64 * k:64 * k + 64]), T.F[:, 1024 * k:1024 * k + 1024], AF.Silu),
-           pcs("F", 2 * k, 2 * k + 2) + ["LA"], pcs("B"))
-    op("v", lambda: V.memset(T.one[:], 1.0), [], ["one"])
-    op("v", lambda: V.memset(T.e14[:], 16384.0), [], ["e14"])
-    dmas("y", "d_xt", [(T.XT[:, w, h], T.x[16 * h + 2 * w::32, :]) for w in range(2) for h in range(2)]
-         + [(T.X1[:, h], T.x[16 * h + 1::32, :]) for h in range(2)], [], ["XT", "X1"])
-    op("g", lambda: g.affine_select(T.I1[:], T.one[:], [[-1, 128]], A.is_equal, 0.0, 0, 1), ["one"], ["I1"])
-    dmas("g", "d_cast", [(T.U[:], T.x[:])], [], ["U"])
-    make_pm(0)
-    op("g", lambda: g.affine_select(T.I14[:], T.e14[:], [[-1, 128]], A.is_equal, 0.0, 0, 1), ["e14"], ["I14"])
+    for z in range(2):
+        iota(T.W[:, 1024 * z:1024 * z + 1024], [[128, 8], [1, 32], [1024, 4]], 128 + 32 * z, 0, [], [("F", z)])
+        if z == 0:
+            for j in range(4):
+                op("g", lambda: g.affine_select(T.PA[:, j, 12:140], T.one[:], [[-16, 8], [-1000, 4], [-4, 4]], A.is_equal, 0.0, -j, 1),
+                   ["one", "PA"], [("PA", j)])
+    dmas("g", "d_q1", [(T.CW[:], T.x[:])], [], ["CW"])
+    copy(T.LN[:], T.oi[:], ["oi"], ["LN"])
+    for z in range(4):
+        copy(T.OF[:, :, z], T.oi[:, 64 * z:64 * z + 64], ["oi"], [("OF", z)])
+    for j in range(4):
+        for y in range(4):
+            mm(T.pL[:, j], T.PA[:, j, 12 - 4 * y:140 - 4 * y], T.OF[:, :, :, :, y], y == 0, y == 3, pcs("OF", 0, 4) + [("PA", j)], "pL")
+    for z in range(2):
+        op("s", lambda: S.activation(T.X1[:, 0:4096].indirect(T.LN[:, 64 * z:64 * z + 64]), T.W[:, 1024 * z:1024 * z + 1024], AF.Silu),
+           [("F", z), "LN", "X1z"], pcs("X1"))
+        op("v", lambda: V.tensor_scalar(T.AO[:].indirect(T.LN[:, 128 + 64 * z:192 + 64 * z]), T.W[:, 0:1024], 1.0, 64.0 + 32 * z,
+                                        A.mult, A.add), [("F", 0), "LN", "AOz"], pcs("AO"))
+        if z == 0:
+            copy(T.LA[:], T.pL[:, 0:4], ["pL"], pcs("LA", 0, 4))
+            send("ra", T.LR[:], T.LA[:], pcs("LA", 0, 4), pcs("LR", 0, 4), -1, "d_l2")
+    dmas("y", "d_b", [(T.DG[:], T.AO[0::16, :]), (T.DC[:], T.X1[0::16, 0:4096])], pcs("AO") + pcs("X1"), ["B1"])
     for h in range(4):
-        op("g", lambda: g.iota(T.cn[32 * h:32 * h + 32, :], [[1, 128]], 0, 128, allow_small_or_imprecise_dtypes=True), [], [("cn", h)])
-    cn = [("cn", h) for h in range(4)]
-    copy("v", T.Ta0[:], T.oi[:], ["oi"], ta_keys(0, 0, 4))
-    op("v", lambda: V.memset(T.big[:], 4096.0), [], ["big"])
-    op("v", lambda: V.memset(T.sel[:], 0.0), [], ["sel"])
-    op("v", lambda: V.memset(T.rst[:], 0.0), [], ["rst"])
-    op("v", lambda: V.memset(T.tie[:], 2.0 ** 17), [], ["tie"])
-    for s in range(4):
-        op("v", lambda: V.memset(T.srow[:, s:256:4], float(s)), [], [("srow", s)] if s < 3 else ["srow"])
-    need("v", ["sel", "rst"], [])
-    cols = [(12 + c, 144, 16) for c in range(4)] + [(152 + c, 288, 16) for c in range(8)] + [(292 + c, 432, 8) for c in range(4)]
-    for i, (c, end, step) in enumerate(cols):
-        op("v", lambda: V.memset(T.sel[:, c:end:step], 2.0 ** 26), [], [("sel", i)] if i < len(cols) - 1 else ["sel"])
-    op("v", lambda: V.memset(T.rst[:, 0:256:4], 2.0 ** 50), [], ["rst"])
-
-    def late_setup():
-        op("v", lambda: V.tensor_scalar(T.cn[:], T.cn[:], EPS, None, A.mult), cn, cn)
-        for h in range(2):
-            op("v", lambda: V.tensor_tensor(T.CT[:, h], T.X1[:, h], T.cn[:], A.add), cn + ["X1"], [("CT", h)])
-        dmas("y", "d_c", [(T.U[16 * h + 1::32, :], T.CT[:, h]) for h in range(2)], [("CT", 0), ("CT", 1)], ["U"])
-        op("v", lambda: V.tensor_scalar(T.nI[:], T.I14[:], -1.0, None, A.mult), ["I14"], ["nI"])
-        copy("v", T.pI[:], T.I14[:], ["I14"], ["pI"])
-
-    def first_b():
-        sl = T.SL[:, 768:1024]
-        ks = [("SL", 3)]
-        return [
-            lambda: op("v", lambda: V.tensor_scalar(sl, T.Tb[:, 0], -128.0, None, A.add), ["Tb"], ks),
-            lambda: op("v", lambda: V.tensor_scalar(sl, sl, 3, None, A.bitwise_and), ks, ks),
-            lambda: op("v", lambda: V.tensor_scalar(T.UT[:, 0], sl, 0.0, 4.0, A.is_equal, A.mult), ks, ["UT"]),
-            lambda: op("v", lambda: V.tensor_tensor(T.Tb[:, 1], T.Tb[:, 0], T.UT[:, 0], A.add), ["Tb", "UT"], ["Tb1"]),
-            lambda: (op("s", lambda: S.activation(T.Tb[:, 0], T.Tb[:, 0], AF.Identity, bias=128.0 - 128.0 * EPS, scale=EPS),
-                        ["Tb", "Tb1"], ["Tb"]),
-                     op("s", lambda: S.activation(T.Tb[:, 1], T.Tb[:, 1], AF.Identity, bias=128.0 - 129.0 * EPS, scale=EPS),
-                        ["Tb1"], ["Tb"]),
-                     round_b(0), put_b(0)),
-        ]
-
-    skip = lambda: None
-    both = lambda *fs: (lambda: run(fs))
-    z0 = lambda q, k: gather(q, "Z", "xb", ["xb", "xb2"], "LA", 0, ["LA"], 2 * k, 2 * k + 2, 128.0)
-    conv_b([0])
-    z0("v", 0)
-    stage("p", 0, 0)
-    z0("v", 1)
-    fill = []
-    for k in range(4):
+        iota(T.cn[32 * h:32 * h + 32, :], [[1, 128]], 128, 128, [], [("cn", h)])
+    op("g", lambda: g.iota(T.pc[:, 0:1], [[0, 1]], 0, 1), [], ["pc"])
+    iota(T.ED[:], [[1, 16], [64, 16]], 0, 0, [], ["ED"])
+    for k in range(8):
+        gather("vs"[k % 2], T.X0[:, 512 * k:512 * k + 512], T.xb[:], T.LA[:, 32 * k:32 * k + 32],
+               ["xb", "xb2", ("LA", k // 2)], [("X0", k)], scale=16384.0)
         if k == 2:
-            late_setup()
-        if k < 3:
-            stage("p", 0, k + 1)
-        scores(0, k, fill)
-        if k < 2:
-            z0("v", k + 2)
-        if k % 2 == 0:
-            choices(0, k // 2, range(4))
-        fill = least(0, k) + pick(0, k, k + 1)
-    run(first_b())
-    for i in range(4):
-        plain_b(i)
-    run(fill)
-    turn_b()
-    list_b(0)
-    make_pm(1)
-    make_rot()
-    ygather("v", 0, 0, 4)
-    ygather("s", 0, 4, 8)
+            op("v", lambda: V.tensor_tensor(T.BD[:], T.DG[:], T.DC[:], A.add), ["B1"], ["BD"] + pcs("DG", 0, 4) + pcs("DC", 0, 4))
+            send("rb", T.BR[:], T.BD[:], ["BD"], ["BR"], -1, "d_l2")
+            dmas("y", "d_cw", [(T.CW[0::16, :], T.BD[:])] + [(T.CW[16 * h + 2::32, :], T.cn[:]) for h in range(2)],
+                 ["BD"] + pcs("cn", 0, 4), ["CW"])
+    dmas("g", "d_q2", [(T.CD[r::4], T.x[r::4, :]) for r in (2, 3)], [], ["CDj"])
+    dmas("y", "d_j", [(T[xname(t)][t::16, 4096:5120], T.DD[0:32, :]) for t in range(RO - 2)], ["zero"], [("X0", "j"), ("X1", "j")])
+    fill(T.KL[:], 0.0, "KL")
+    fill(T.TL[:], 0.0, "TL")
+    fill(T.TR[:], 0.0, "TR")
+    fill(T.SEL[:], 0.0, "SEL")
+    fill(T.rst[:], 0.0, "rst")
+    fill(T.KR[:], 2.0 ** 21, "KR")
+    fill(T.UL[:, :, 8::9], 0.0, "UL")
+    for r in (0, 64):
+        fill(T.TL[r:r + 1], 1.0, "TL")
+    fill(T.TR[96:97], 1.0, "TR")
+    fill(T.KL[64:65], 0.5, "KL")
+    fill(T.SEL[:, :, 0:144:16], -4096.0, "SEL")
+    for p in range(4):
+        fill(T.SEL[:, p, 2 ** p:144:16], -4096.0, "SEL")
+    fill(T.rst[:, :, 0::4], BIG, "rst")
+    fill(T.rst[:, 1, 1::2], 512.0, "rst")
+    fill(T.rst[:, 1, 2::4], -512.0, "rst")
+    iota(T.TL[96:97], [[0, 32], [1, 16]], 0, 0, [], ["TL"])
+    iota(T.TR[0:1, 0:9], [[0, 288], [1280, 4]], 0, 0, [], ["TR"])
+    const_low(0)
+    op("v", lambda: V.tensor_scalar(T.pc[:, 1:2], T.pc[:, 0:1], 3, None, A.bitwise_and), ["pc"], ["pc1"])
+    op("v", lambda: V.tensor_scalar(T.pc[:, 2:3], T.pc[:, 0:1], 12, None, A.bitwise_and), ["pc"], ["pc2"])
+    op("v", lambda: V.tensor_scalar(T.pf[:, 1:2], T.pc[:, 1:2], 1024.0, None, A.mult), ["pc1"], ["pf1"])
+    op("v", lambda: V.tensor_scalar(T.pf[:, 2:3], T.pc[:, 2:3], 4.0, None, A.mult), ["pc2"], ["pf2"])
+    op("v", lambda: V.tensor_scalar(T.EC[:], T.ED[:], T.pf[:, 1:2], T.pf[:, 2:3], A.add, A.add), ["ED", "pf1", "pf2"], ["EC"])
+    turned(1)
+    dmas("y", "d_cw", [(T.CW[1::16, :], T.BR[:])], ["BR"], ["CW"])
 
-    for t in range(1, RO):
-        last = t == RO - 1
-        bgather("v", t, 0, 4)
-        bgather("s", t, 4, 8)
-        conv_b([0, 1])
-        fgather("v", t, 0, 4)
-        fgather("s", t, 4, 8)
-        lk = [least(t, k) for k in range(4)]
-        tr = [lambda k=k: turn_a(t, k) for k in range(4)]
-        ch = [[lambda u=u, s=s: choices(t, u, [s]) for s in range(4)] for u in range(2)]
-        p01, p2, p3 = pick(t, 0, 2), pick(t, 2, 3), pick(t, 3, 4)
-        pl = [lambda i=i: plain_b(i) for i in range(4)]
-        zgather("v", t, 0, 1)
-        zgather("s", t, 2, 3)
-        if t < 2:
-            zgather("v", t, 1, 2)
-        stage("s", t, 0)
-        if t >= 2:
-            zgather("v", t, 1, 2)
-        conv_a(0)
-        zgather("s", t, 3, 4)
-        conv_a(1)
-        round_b(t)
-        scores(t, 0, [])
-        stage("s", t, 1)
-        zgather("s", t, 4, 6)
-        conv_a(2)
-        round_a(0)
-        zgather("s", t, 6, 7)
-        round_a(1)
-        scores(t, 1, [skip] * 3 + lk[0] + [tr[0], both(tr[1], ch[0][0], ch[0][1])])
-        stage("s", t, 2)
-        zgather("s", t, 7, 8)
-        conv_a(3)
-        if last:
-            for k in range(4):
-                conv_last(k)
-        put_b(t)
-        scores(t, 2, [both(ch[0][2], ch[0][3]), lk[1][0], both(lk[1][1], pl[0]), pl[1]]
-               + [both(p01[0], pl[2]), both(p01[1], pl[3])] + p01[2:])
-        stage("s", t, 3)
-        round_a(2)
-        round_a(3)
-        scores(t, 3, [lk[2][0], lk[2][1], both(tr[2], tr[3], ch[1][0], ch[1][1]), skip, both(ch[1][2], ch[1][3])])
-        ygather("s", t, 0, 4)
-        if last:
-            list_last()
-        run([p2[0], turn_b, p2[1], lk[3][0]] + p2[2:3] + [lk[3][1]] + p2[3:] + p3)
-        list_b(t)
-        if not last:
-            list_a(t)
-        if t <= 4:
-            places(2 * t - 2)
-            places(2 * t - 1)
-        ygather("v", t, 4, 5)
-        ygather("s", t, 5, 6)
-        ygather("v", t, 6, 7)
-        ygather("s", t, 7, 8)
+    def first_maps():
+        for k in range(8):
+            gather("vs"[k % 2], T.W[:, 512 * k:512 * k + 512], T.CW[:], T.LA[:, 32 * k:32 * k + 32],
+                   ["CW", ("LA", k // 2)], [("W", k), ("F", k // 2)], add=-128.0)
+        extract("W", 1, "EC")
+        turned(0)
 
-    fgather("v", RO, 0, 4)
-    copy("v", T.LA[:], T.pE[:, 4:8], ["pE"], ["LA"])
-    fgather("s", RO, 4, 8)
-    zgather("v", RO, 0, 4)
-    zgather("s", RO, 4, 8)
-    dmas("y", "d_out", [(T.yo[:], T.Z[0::16, :])], pcs("Z"), [])
+    order = [(0, 0), (0, 1), (1, 0), (1, 1), (0, 2), (1, 2), (2, 0), (2, 1), (2, 2), (0, 3), (1, 3), (2, 3), (3, 0), (3, 1), (3, 2), (3, 3)]
+    for t in range(RO):
+        first, last = t == 0, t == RO - 1
+        cs = [(k, u) for k in range(4) for u in range(4)]
+
+        def c_some(q, cnt):
+            for _ in range(cnt):
+                k, u = cs.pop(0)
+                c_piece(q, "LR" if first else "LG", k, u, -128.0 if first else None)
+                if u == 3 and k < 3:
+                    c_dense(k)
+
+        def carried():
+            if not first:
+                strip_v()
+                turned(0)
+
+        if not first:
+            extract(xname(t), 15 if last else t - 1, "ED")
+        if POS[t] <= 4:
+            narrow_low("v", t, 0, 0, range(8))
+            narrow_low("s", t, 0, 1, range(8))
+            if first:
+                first_maps()
+            narrow_low("s", t, 1, 0, range(8))
+            if not first:
+                strip_s()
+            narrow_low("s", t, 1, 1, range(8))
+            if first:
+                dmas("g", "d_ac", [(T.X0[15::16, 0:4096], T.W[2::16, 0:4096])], pcs("W"), pcs("X0"), accum_op=A.add, max_dma_last_dim=4096)
+            for j in range(4):
+                scan_low(t, 0, j)
+                if j == 2:
+                    carried()
+            c_some("s", 12)
+            for j in range(4):
+                scan_low(t, 1, j)
+                if j == 1 and POS[t] < 4:
+                    offsets_low(t, 0)
+            c_list(0)
+            offsets_low(t, 1)
+        else:
+            narrow_high("v", t, 0, 0)
+            narrow_high("s", t, 1, 0)
+            narrow_high("s", t, 1, 1)
+            narrow_high("v", t, 0, 1)
+            narrow_high("s", t, 1, 2)
+            narrow_high("s", t, 0, 2)
+            strip_s()
+            narrow_high("s", t, 1, 3)
+            narrow_high("s", t, 0, 3)
+            for i, (j, jj) in enumerate(order):
+                scan_high(i, j, jj)
+                if i == 6:
+                    carried()
+            c_some("s", 12)
+            c_list(0)
+            offsets_high(t)
+        for u in range(4):
+            select("vs"[u % 2], t, u)
+        spread(t)
+        c_some("v", 2)
+        c_some("s", 2)
+        c_dense(3)
+        c_list(1)
+        for k in range(4):
+            if k >= 2:
+                c_list(k)
+            a_piece("v", 2 * k)
+            a_piece("s", 2 * k + 1)
+            a_dense("DD", "d_d%d" % k, 0, k, k + 1)
+            if k == 2:
+                d_send(t, 0)
+        for k in range(1, 4):
+            d_send(t, k)
+        if last:
+            break
+        di = "DI%d" % (t % 2)
+        dmas("y", "d_i", [(T[di][:], T.AO[1::16, :])], pcs("AO"), [di])
+        send("n%d" % t, T["IR%d" % t][:], T[di][:], [di], [("IR", t)], 1, "d_l2")
+        a_dense("DG", "d_g0", 2, 0, 4)
+        if t < 3:
+            const_low(t + 1)
+        if t == 3:
+            const_high()
+        if t == 4:
+            const_high_v()
+        if t < RO - 2:
+            copy(T.LG[:], T.DG[:], pcs("DG", 0, 4), pcs("LG", 0, 4))
+        else:
+            for y in range(4):
+                for j in range(4):
+                    mm(T.pR[:, 0, :, :, :, y], T.PB[:, y, 3 - j:131 - j], T.DG[:, 64 * j:64 * j + 64], j == 0, j == 3,
+                       pcs("DG", 0, 4) + [("PB", y), "PB"], "pR")
+        for k in range(8):
+            b_piece("vs"[k % 2], t, k)
+            if k == 4 and t == RO - 2:
+                for z in range(4):
+                    copy(T.LG[:, 64 * z:64 * z + 64], T.pR[:, 0, :, z], ["pR"], [("LG", z)])
+        dmas("y", "d_cw", [(T.CW[0::16, :], T["IR%d" % t][:])], [("IR", t)], ["CW"])
+
+    for k in range(4):
+        dmas("y", "d_out", [(T.yo[:, 64 * k:64 * k + 64], T.YR[:, 64 * k:64 * k + 64])], [("YR", k)], [])
     for sem, cnt in total.items():
         g.wait_ge(T.sem[sem], cnt)

@@ -3,6 +3,8 @@ from concourse.mybir import dt, AluOpType, AxisListType, ActivationFunctionType
 RO = 8
 POS = [0, 1, 2, 3, 4, 7, 8, 9]
 BIG = 2.0 ** 40
+NS = 10
+AV = [32, 26, 32, 26]
 
 SCRATCH = {
     "X0": ("sbuf", [128, 5120], "float32"),
@@ -38,13 +40,14 @@ SCRATCH = {
     "cn": ("sbuf", [128, 128], "float32"),
     "one": ("sbuf", [128, 128], "float32"),
     "SEL": ("sbuf", [128, 5, 144], "bfloat16"),
-    "KL": ("sbuf", [128, 4, 128], "bfloat16"),
-    "KR": ("sbuf", [128, 128], "bfloat16"),
-    "TL": ("sbuf", [128, 4, 128], "bfloat16"),
-    "TR": ("sbuf", [128, 11, 128], "bfloat16"),
-    "rst": ("sbuf", [128, 2, 128], "float32"),
-    "SL": ("sbuf", [128, 2, 128], "int32"),
-    "SA": ("sbuf", [128, 2, 32], "int32"),
+    "KL": ("sbuf", [128, 128], "bfloat16"),
+    "KR": ("sbuf", [128, 256], "bfloat16"),
+    "TL": ("sbuf", [128, 128], "bfloat16"),
+    "TR": ("sbuf", [128, 256], "bfloat16"),
+    "rs0": ("sbuf", [128, 256], "float32"),
+    "rs1": ("sbuf", [128, 128], "float32"),
+    "SL": ("sbuf", [128, 256], "int32"),
+    "SA": ("sbuf", [128, 64], "int32"),
     "RI": ("sbuf", [128, 2, 2, 2, 8], "int32"),
     "RB": ("sbuf", [128, 64], "bfloat16"),
     "idn": ("sbuf", [128, 128], "bfloat16"),
@@ -57,13 +60,12 @@ SCRATCH = {
     "PA": ("sbuf", [128, 4, 144], "float32"),
     "PB": ("sbuf", [128, 4, 132], "float32"),
     "pK0": ("psum", [128, 512], "float32"),
-    "pK1": ("psum", [128, 512], "float32"),
     "pL": ("psum", [128, 8, 64], "float32"),
     "pR": ("psum", [128, 2, 8, 4, 2, 4], "float32"),
     "pS": ("psum", [128, 512], "float32"),
 }
 for _t in range(RO - 1):
-    SCRATCH["DS%d" % (_t % 2)] = ("sbuf", [128, 256], "uint16")
+    SCRATCH["DS%d" % _t] = ("sbuf", [128, 256], "uint16")
     SCRATCH["DI%d" % (_t % 2)] = ("sbuf", [128, 256], "float32")
     SCRATCH["LD%d" % _t] = ("sbuf", [128, 256], "uint16")
     SCRATCH["IR%d" % _t] = ("sbuf", [128, 256], "float32")
@@ -163,8 +165,8 @@ def rank_program(g, core, T, topo):
     def copy(o_, i_, reads, writes):
         op("v", lambda: V.tensor_copy(o_, i_), reads, writes)
 
-    def fill(ap, val, key):
-        op("v", lambda: V.memset(ap, val), [], [key])
+    def fill(ap, val, key, after=()):
+        op("v", lambda: V.memset(ap, val), list(after), [key])
 
     def iota(ap, pattern, base, cm, reads, writes):
         op("g", lambda: g.iota(ap, pattern, base, cm, allow_small_or_imprecise_dtypes=True), reads, writes)
@@ -175,8 +177,9 @@ def rank_program(g, core, T, topo):
     def xname(t):
         return "X%d" % (t % 2)
 
-    def a_piece(q, k):
-        gather(q, T.AO[:, 512 * k:512 * k + 512], T.W[:, 0:4096], T.LC[:, 32 * k:32 * k + 32], ["W", ("LC", k // 2)], [("AO", k)])
+    def a_piece(q, k, c0, c1):
+        gather(q, T.AO[:, 1024 * k + 16 * c0:1024 * k + 16 * c1], T.W[:, 0:4096], T.LC[:, 64 * k + c0:64 * k + c1], ["W", ("LC", k)],
+               [("AO", 2 * k + (c0 > 0))])
 
     def b_piece(q, t, k):
         x, y = xname(t), xname(t + 1)
@@ -191,15 +194,15 @@ def rank_program(g, core, T, topo):
         dmas("y", "d_c%d" % k, [(T.DC[:, 64 * k:64 * k + 64], T.CO[0::16, 1024 * k:1024 * k + 1024])],
              [("CO", k, u) for u in range(4)], [("DC", k)])
 
-    def c_list(k):
-        copy(T.LC[:, 64 * k:64 * k + 64], T.DC[:, 64 * k:64 * k + 64], [("DC", k)], [("LC", k)])
+    def c_list(k0, k1):
+        copy(T.LC[:, 64 * k0:64 * k1], T.DC[:, 64 * k0:64 * k1], pcs("DC", k0, k1), pcs("LC", k0, k1))
 
     def a_dense(name, sem, row, k0, k1):
         dmas("y", sem, [(T[name][:, 64 * k:64 * k + 64], T.AO[row::16, 1024 * k:1024 * k + 1024]) for k in range(k0, k1)],
              pcs("AO", 2 * k0, 2 * k1), [(name, k) for k in range(k0, k1)] + ["zero"] * (name == "DD" and k0 == 0))
 
     def d_send(t, k):
-        ds = "DS%d" % (t % 2)
+        ds = "DS%d" % t
         cols = slice(64 * k, 64 * k + 64)
         if t == RO - 1:
             send("m%d_%d" % (t, k), T.YR[:, cols], T.DD[:, cols], [("DD", k)], [("YR", k)])
@@ -207,8 +210,8 @@ def rank_program(g, core, T, topo):
         copy(T[ds][:, cols], T.DD[:, cols], [("DD", k)], [(ds, k)])
         send("m%d_%d" % (t, k), T["LD%d" % t][:, cols], T[ds][:, cols], [(ds, k)], [("LD", t, k)])
 
-    def extract(name, row, dst):
-        dmas("y", "d_ex", [(T[dst][j::4, :], T[name][row::16, 1024 * j:1024 * j + 1024]) for j in range(4)], pcs(name), [dst])
+    def extract(name, row):
+        dmas("y", "d_ex", [(T.ED[j::4, :], T[name][row::16, 1024 * j:1024 * j + 1024]) for j in range(4)], pcs(name), ["ED"])
 
     def strip_s():
         op("s", lambda: S.activation(T.EH[:], T.ED[:], AF.Identity, bias=128.0, scale=2.0 ** -14), ["ED"], ["EH"])
@@ -217,13 +220,17 @@ def rank_program(g, core, T, topo):
     def strip_v():
         op("v", lambda: V.tensor_tensor(T.EC[:], T.ED[:], T.pS[:, 0:256], A.add), ["ED", "pS"], ["EC"])
 
-    def turned(row):
-        dmas("y", "d_cd", [(T.CD[4 * j + row::16, :, 256 * r:256 * r + 256], T.EC[(j + r) % 4::4, :])
-                           for r in range(4) for j in range(4)], ["EC"], ["CD"])
+    def table(j):
+        return T.EC[j::4, :]
+
+    def turned(row, src, keys):
+        dmas("y", "d_cd", [(T.CD[4 * j + row::16, :, 256 * r:256 * r + 256], src((j + r) % 4))
+                           for r in range(4) for j in range(4)], keys, [("CD", row)])
 
     def select(q, t, u):
         far = u ^ (2 ** (POS[t] - 8)) if POS[t] >= 8 else u
-        gather(q, T.TH[:, 256 * u:256 * u + 256], T.CD[:, far, :], T.LS[:, 16 * u:16 * u + 16], ["CD", "CDj", "LS0", "LS1"], [("TH", u)])
+        gather(q, T.TH[:, 256 * u:256 * u + 256], T.CD[:, far, :], T.LS[:, 16 * u:16 * u + 16],
+               [("CD", 0), ("CD", 1), "CDj", "LS0", "LS1"], [("TH", u)])
 
     def spread(t):
         th = pcs("TH", 0, 4)
@@ -242,58 +249,77 @@ def rank_program(g, core, T, topo):
         else:
             op(q, lambda: S.activation(o_, i_, AF.Identity, bias=128.0 + 16 * m, scale=2.0 ** -14), reads, writes)
 
-    def low_bits(p, b, m, h):
-        if p == 4:
-            return 16 * b + 8 * h + m
-        return 16 * h + ((m >> p) << (p + 1)) + (b << p) + (m & (2 ** p - 1))
+    def around(p, b, m):
+        return ((m >> p) << (p + 1)) + (b << p) + (m & (2 ** p - 1))
 
-    def narrow_low(q, t, h, b, ms):
+    ties = ["TL", "TR", "TL32", "TR0", "TR32", "TR64"]
+
+    def open_keys(wd):
+        mm(T.pK0[:, 0:wd], T.KL[:], T.KR[:, 0:wd], True, False, ["KL", "KL0", "KL32", "KR"], "pK0")
+
+    def close_keys(wd):
+        mm(T.pK0[:, 0:wd], T.TL[:], T.TR[:, 0:wd], False, True, ties, "pK0")
+
+    def least(rs, c0, wd):
+        op("v", lambda: V.tensor_tensor_scan(T.SL[:, c0:c0 + wd], T[rs][:, 0:wd], T.pK0[:, 0:wd], 0.0, A.add, A.min), [rs, "pK0"], [("SL", c0)])
+
+    def narrow_low(q, t, b, jp):
         x = xname(t)
-        for m in ms:
-            narrow(q, T.UL[:, 2 * h + b, m::9], T[x][:, low_bits(POS[t], b, m, h):4096:32], m, pcs(x) + ["UL"], [("UL", h, b, m)])
+        for m in range(8):
+            c0 = 2048 * jp + around(POS[t], b, m)
+            narrow(q, T.UL[:, 2 * jp + b, m::9], T[x][:, c0:2048 * jp + 2048:16], m, pcs(x, 4 * jp, 4 * jp + 4) + ["UL"], [("UL", jp, b, m)])
 
-    def scan_low(t, h, j):
+    def scan_low(t, i, j, jj):
         p = POS[t]
-        bank = "pK%d" % (h if p < 4 else 0)
+        s = (jj - j) % 4
+        side = lambda b, y: T.UL[:, 2 * (y // 2) + b, 576 * (y % 2):576 * (y % 2) + 576]
+        if i == 0:
+            open_keys(256)
+        op("v", lambda: V.tensor_tensor_scan(T.MH[:, i % 4, 0:576], side(0, j), side(1, jj), 0.0, A.max, A.min),
+           [("UL", y // 2, b, m) for b, y in ((0, j), (1, jj)) for m in range(8)], [("MH", i % 4)])
+        for m in range(8):
+            c0 = around(p, 0, m)
+            mm(T.pK0[:, s:256:4], T.SEL[:, p, 16 - c0:144 - c0], T.MH[:, i % 4, m:576:9], False, False, [("MH", i % 4), "SEL", ("SEL", p)], "pK0")
+        if i == 15:
+            close_keys(256)
+
+    def offsets_low():
+        least("rs0", 0, 256)
+        op("v", lambda: V.tensor_scalar(T.SA[:], T.SL[:, 3::4], 1023, None, A.bitwise_and), [("SL", 0)], ["SA"])
+        copy(T.LS[:], T.SA[:], ["SA"], ["LS0", "LS1"])
+
+    def narrow_mid(q, t, h, b):
+        x = xname(t)
+        for m in range(8):
+            narrow(q, T.UL[:, 2 * h + b, m::9], T[x][:, 16 * b + 8 * h + m:4096:32], m, pcs(x) + ["UL"], [("UL", h, b, m)])
+
+    def scan_mid(h, j):
         rd = [("UL", h, b, m) for b in range(2) for m in range(8)]
-        if j == 0 and (p < 4 or h == 0):
-            mm(T[bank][:, 0:128], T.KL[:, min(p, 3)], T.KR[:], True, False, [("KL", min(p, 3)), "KR"], bank)
+        if j == 0 and h == 0:
+            open_keys(128)
         for s in range(4):
             jj = (j + s) % 4
             op("v", lambda: V.tensor_tensor_scan(T.ML[:, h, 288 * j:288 * j + 288, s], T.UL[:, 2 * h, 288 * j:288 * j + 288],
                                                  T.UL[:, 2 * h + 1, 288 * jj:288 * jj + 288], 0.0, A.max, A.min), rd, [("ML", h, j, s)])
         for m in range(8):
-            c0 = low_bits(p, 0, m, h) % 16
-            mm(T[bank][:, 0:128], T.SEL[:, p, 16 - c0:144 - c0], T.ML[:, h, 288 * j + m:288 * j + 288:9, :], False, False,
-               [("ML", h, j, s) for s in range(4)] + ["SEL"], bank)
-        if j == 3 and (p < 4 or h == 1):
-            r = 2 * p + h if p < 4 else 8
-            mm(T[bank][:, 0:128], T.TL[:, min(p, 3)], T.TR[:, r], False, True, [("TL", min(p, 3)), ("TR", r), "TL", "TR"], bank)
+            c0 = 8 * h + m
+            mm(T.pK0[:, 0:128], T.SEL[:, 4, 16 - c0:144 - c0], T.ML[:, h, 288 * j + m:288 * j + 288:9, :], False, False,
+               [("ML", h, j, s) for s in range(4)] + ["SEL"], "pK0")
+        if j == 3 and h == 1:
+            close_keys(128)
 
-    def least(w, h, bank):
-        op("v", lambda: V.tensor_tensor_scan(T.SL[:, h], T.rst[:, w], T[bank][:, 0:128], 0.0, A.add, A.min), ["rst", bank], [("SL", h)])
-
-    def offsets_low(t, h):
-        if POS[t] < 4:
-            least(0, h, "pK%d" % h)
-            hs = [h]
-        else:
-            least(1, 1, "pK0")
-            least(0, 0, "pK0")
-            op("v", lambda: V.tensor_scalar(T.SL[:, 1, 3::4], T.SL[:, 1, 3::4], -272.0, None, A.add), [("SL", 1)], [("SL", 1)])
-            hs = [0, 1]
-        h0, h1 = hs[0], hs[-1] + 1
-        op("v", lambda: V.tensor_scalar(T.SA[:, h0:h1], T.SL[:, h0:h1, 3::4], 1023, None, A.bitwise_and),
-           [("SL", k) for k in hs], [("SA", k) for k in hs])
-        for k in hs:
-            copy(T.LS[:, k::2], T.SA[:, k], [("SA", k)], ["LS%d" % k])
+    def offsets_mid():
+        least("rs1", 128, 128)
+        least("rs0", 0, 128)
+        op("v", lambda: V.tensor_scalar(T.SL[:, 131::4], T.SL[:, 131::4], -272.0, None, A.add), [("SL", 128)], [("SL", 128)])
+        op("v", lambda: V.tensor_scalar(T.SA[:], T.SL[:, 3::4], 1023, None, A.bitwise_and), [("SL", 0), ("SL", 128)], ["SA"])
+        for b in range(2):
+            copy(T.LS[:, b::2], T.SA[:, 32 * b:32 * b + 32], ["SA"], ["LS%d" % b])
 
     def narrow_high(q, t, b, j):
         x = xname(t)
-        e = POS[t] - 7
         for m in range(4):
-            top = ((m >> e) << (e + 1)) + (b << e) + (m & (2 ** e - 1))
-            c0 = 1024 * j + 128 * top
+            c0 = 1024 * j + 128 * around(POS[t] - 7, b, m)
             narrow(q, T.UH[:, 4 * b + j, m::5], T[x][:, c0:c0 + 128], m, pcs(x, 2 * j, 2 * j + 2) + ["UH"], [("UH", b, j, m)])
 
     def scan_high(i, j, jj):
@@ -308,27 +334,47 @@ def rank_program(g, core, T, topo):
     def offsets_high(t):
         e = POS[t] - 7
         side = lambda b: [T.RI[:, :, :, b, :], T.RI[:, :, b, :, :], T.RI[:, b, :, :, :]][e]
-        r = 9 if e == 0 else 10
-        mm(T.pL[:, 0], T.TL[:, 0], T.TR[:, r, 0:64], True, False, [("TL", 0), ("TR", r), "TL", "TR"], "pL")
-        least(0, 0, "pK0")
-        op("v", lambda: V.tensor_scalar(side(0), T.SL[:, 0, 3::4], 2, 3, A.logical_shift_right, A.bitwise_and), [("SL", 0)], ["RI0"])
-        op("v", lambda: V.tensor_scalar(side(1), T.SL[:, 0, 3::4], 3, None, A.bitwise_and), [("SL", 0)], ["RI1"])
+        mm(T.pL[:, 0], T.TL[:], T.TR[:, 0:64], True, False, ties, "pL")
+        least("rs0", 0, 128)
+        op("v", lambda: V.tensor_scalar(side(0), T.SL[:, 3:128:4], 2, 3, A.logical_shift_right, A.bitwise_and), [("SL", 0)], ["RI0"])
+        op("v", lambda: V.tensor_scalar(side(1), T.SL[:, 3:128:4], 3, None, A.bitwise_and), [("SL", 0)], ["RI1"])
         copy(T.RB[:], T.RI[:], ["RI0", "RI1"], ["RB"])
         mm(T.pL[:, 0], T.S16[:], T.RB[:], False, True, ["S16", "RB"], "pL")
         copy(T.LS[:], T.pL[:, 0], ["pL"], ["LS0", "LS1"])
 
-    def const_low(p):
-        iota(T.KL[0:1, p], [[0, 128 // 2 ** p], [16, 2 ** p]], 135, 0, ["KL"], [("KL", p, 0)])
-        iota(T.KL[32:33, p], [[0, 8], [16 * 2 ** p, 8 // 2 ** p], [0, 2 ** (p + 1)]], 0, 0, ["KL", ("KL", p, 0)], [("KL", p)])
-        iota(T.TL[32:33, p], [[0, 64 // 2 ** p], [1, 2], [0, 2 ** p]], 0, 0, ["TL"], [("TL", p)])
-        iota(T.TR[32:33, 2 * p:2 * p + 2], [[0, 128], [-512, 2]], 256 - 2 ** (p + 1), 0, ["TR"], [("TR", p, 0)])
-        for h in range(2):
-            iota(T.TR[64:65, 2 * p + h], [[0, 4], [32, 8], [0, 4]], 16 * h + 2 ** p, 0, ["TR", ("TR", p, 0)], [("TR", 2 * p + h)])
+    def const_round(t):
+        p = POS[t]
+        if p < 4:
+            iota(T.KL[0:1], [[0, 128 // 2 ** p], [16, 2 ** p]], 135, 0, ["KL"], ["KL0"])
+            iota(T.KL[32:33], [[0, 8], [16 * 2 ** p, 8 // 2 ** p], [0, 2 ** (p + 1)]], 0, 0, ["KL"], ["KL32"])
+            iota(T.TL[32:33], [[0, 64 // 2 ** p], [1, 2], [0, 2 ** p]], 0, 0, ["TL"], ["TL32"])
+            iota(T.TR[32:33], [[0, 128], [-512, 2]], 256 - 2 ** (p + 1), 0, ["TR"], ["TR32"])
+            iota(T.TR[64:65], [[0, 4], [16, 16], [0, 4]], 2 ** p, 0, ["TR"], ["TR64"])
+        elif p == 4:
+            iota(T.TR[32:33, 0:128], [[0, 128]], 0, 0, ["TR"], ["TR32"])
+            iota(T.TR[64:65, 0:128], [[0, 4], [32, 8], [0, 4]], 16, 0, ["TR"], ["TR64"])
+        elif p == 7:
+            iota(T.TR[0:1, 0:64], [[0, 64]], 0, 0, ["TR"], ["TR0"])
+            iota(T.TR[64:65, 0:64], [[0, 4], [-128, 2], [16, 8]], 128, 0, ["TR"], ["TR64"])
+        elif p == 8:
+            iota(T.TR[64:65, 0:64], [[0, 4], [128, 2], [16, 8]], 0, 0, ["TR"], ["TR64"])
+
+    def const_round_v(t):
+        if POS[t] < 4:
+            fill(T.SEL[:, POS[t], 2 ** POS[t]:144:16], -4096.0, ("SEL", POS[t]), ["SEL"])
+        if POS[t] == 3:
+            fill(T.rs1[:], 512.0, "rs1")
+            fill(T.rs1[:, 0::4], BIG, "rs1")
+            fill(T.rs1[:, 2::4], -512.0, "rs1")
+        if POS[t] == 4:
+            fill(T.m16[:], -16.0, "m16")
+            fill(T.UH[:, :, 4::5], 0.0, "UH")
+            fill(T.PB[:, :, 0:3], 0.0, "PB")
+        if POS[t] == 7:
+            op("v", lambda: V.tensor_scalar(T.tmp[:], T.tmp[:], 15, None, A.bitwise_and), ["tmp"], ["tmp"])
+            op("v", lambda: V.tensor_scalar(T.S16[:], T.tmp[:], 0.0, 256.0, A.is_equal, A.mult), ["tmp"], ["S16"])
 
     def const_high():
-        iota(T.TR[64:65, 8], [[0, 4], [32, 8], [0, 4]], 16, 0, ["TR"], [("TR", 8)])
-        iota(T.TR[64:65, 9, 0:64], [[0, 4], [-128, 2], [16, 8]], 128, 0, ["TR"], [("TR", 9)])
-        iota(T.TR[64:65, 10, 0:64], [[0, 4], [128, 2], [16, 8]], 0, 0, ["TR"], [("TR", 10)])
         op("g", lambda: g.affine_select(T.idn[:], T.one[:], [[-1, 128]], A.is_equal, 0.0, 0, 1), ["one"], ["idn"])
         iota(T.MS[:], [[0, 32], [10, 2], [3, 2]], 1, 0, [], ["MS"])
         op("g", lambda: g.affine_select(T.MS[:], T.MS[:], [[0, 4], [-16, 8], [0, 4]], A.is_ge, 0.0, 0, 1), ["MS"], ["MS"])
@@ -338,27 +384,29 @@ def rank_program(g, core, T, topo):
             op("g", lambda: g.affine_select(T.PB[:, y, 3:131], T.one[:], [[-16, 8], [-1, 4], [-1000, 4]], A.is_equal, 0.0, -4 * y, 1),
                ["one", "PB"], [("PB", y)])
 
-    def const_high_v():
-        op("v", lambda: V.tensor_scalar(T.tmp[:], T.tmp[:], 15, None, A.bitwise_and), ["tmp"], ["tmp"])
-        op("v", lambda: V.tensor_scalar(T.S16[:], T.tmp[:], 0.0, 256.0, A.is_equal, A.mult), ["tmp"], ["S16"])
-        fill(T.m16[:], -16.0, "m16")
-        fill(T.UH[:, :, 4::5], 0.0, "UH")
-        fill(T.PB[:, :, 0:3], 0.0, "PB")
-
     dmas("y", "d_o", [(T.oi[:], T.o[:])], [], ["oi"])
     fill(T.DD[:], 0.0, "zero")
     fill(T.one[:], 1.0, "one")
-    fill(T.PA[:, :, 0:12], 0.0, "PA")
     dmas("y", "d_z", [(T.AO[0::16, :], T.DD[:]), (T.X1[0::16, 0:4096], T.DD[:])], ["zero"], ["AOz", "X1z"])
     dmas("y", "d_x", [(T.xb[:, 0:2048], T.x[:, 0:2048])], [], ["xb"])
     dmas("s", "d_x", [(T.xb[:, 2048:4096], T.x[:, 2048:4096])], [], ["xb2"])
+    fill(T.PA[:, :, 0:12], 0.0, "PA")
+    fill(T.KL[:], 0.0, "KLz")
+    fill(T.TL[:], 0.0, "TLz")
+    fill(T.TR[:], 0.0, "TRz")
+    fill(T.SEL[:], 0.0, "SELz")
+    fill(T.KR[:], 2.0 ** 21, "KR")
+    fill(T.KL[64:65], 0.5, "KL", ["KLz"])
+    fill(T.TL[0:1], 1.0, "TL0", ["TLz"])
+    fill(T.TL[64:65], 1.0, "TL64", ["TLz"])
+    fill(T.TR[96:97], 1.0, "TR", ["TRz"])
     for z in range(2):
         iota(T.W[:, 1024 * z:1024 * z + 1024], [[128, 8], [1, 32], [1024, 4]], 128 + 32 * z, 0, [], [("F", z)])
         if z == 0:
-            for j in range(4):
-                op("g", lambda: g.affine_select(T.PA[:, j, 12:140], T.one[:], [[-16, 8], [-1000, 4], [-4, 4]], A.is_equal, 0.0, -j, 1),
-                   ["one", "PA"], [("PA", j)])
-    dmas("g", "d_q1", [(T.CW[:], T.x[:])], [], ["CW"])
+            dmas("g", "d_q1", [(T.CW[:], T.x[:])], [], ["CW"])
+    for j in range(4):
+        op("g", lambda: g.affine_select(T.PA[:, j, 12:140], T.one[:], [[-16, 8], [-1000, 4], [-4, 4]], A.is_equal, 0.0, -j, 1),
+           ["one", "PA"], [("PA", j)])
     copy(T.LN[:], T.oi[:], ["oi"], ["LN"])
     for z in range(4):
         copy(T.OF[:, :, z], T.oi[:, 64 * z:64 * z + 64], ["oi"], [("OF", z)])
@@ -370,60 +418,61 @@ def rank_program(g, core, T, topo):
            [("F", z), "LN", "X1z"], pcs("X1"))
         op("v", lambda: V.tensor_scalar(T.AO[:].indirect(T.LN[:, 128 + 64 * z:192 + 64 * z]), T.W[:, 0:1024], 1.0, 64.0 + 32 * z,
                                         A.mult, A.add), [("F", 0), "LN", "AOz"], pcs("AO"))
-        if z == 0:
-            copy(T.LA[:], T.pL[:, 0:4], ["pL"], pcs("LA", 0, 4))
-            send("ra", T.LR[:], T.LA[:], pcs("LA", 0, 4), pcs("LR", 0, 4), -1, "d_l2")
     dmas("y", "d_b", [(T.DG[:], T.AO[0::16, :]), (T.DC[:], T.X1[0::16, 0:4096])], pcs("AO") + pcs("X1"), ["B1"])
+    copy(T.LA[:], T.pL[:, 0:4], ["pL"], pcs("LA", 0, 4))
     for h in range(4):
         iota(T.cn[32 * h:32 * h + 32, :], [[1, 128]], 128, 128, [], [("cn", h)])
     op("g", lambda: g.iota(T.pc[:, 0:1], [[0, 1]], 0, 1), [], ["pc"])
     iota(T.ED[:], [[1, 16], [64, 16]], 0, 0, [], ["ED"])
+    iota(T.TL[96:97], [[0, 8], [1, 16]], 0, 0, ["TL0", "TL64"], ["TL"])
+    iota(T.TR[0:1], [[0, 64], [1280, 4]], 0, 0, ["TR"], ["TR0"])
+    dmas("y", "d_cw", [(T.CW[16 * h + 2::32, :], T.cn[:]) for h in range(2)], pcs("cn", 0, 4), ["CW"])
+    send("ra", T.LR[:], T.LA[:], pcs("LA", 0, 4), pcs("LR", 0, 4), -1, "d_l2")
     for k in range(8):
-        gather("vs"[k % 2], T.X0[:, 512 * k:512 * k + 512], T.xb[:], T.LA[:, 32 * k:32 * k + 32],
+        gather("vsvssvss"[k], T.X0[:, 512 * k:512 * k + 512], T.xb[:], T.LA[:, 32 * k:32 * k + 32],
                ["xb", "xb2", ("LA", k // 2)], [("X0", k)], scale=16384.0)
         if k == 2:
             op("v", lambda: V.tensor_tensor(T.BD[:], T.DG[:], T.DC[:], A.add), ["B1"], ["BD"] + pcs("DG", 0, 4) + pcs("DC", 0, 4))
             send("rb", T.BR[:], T.BD[:], ["BD"], ["BR"], -1, "d_l2")
-            dmas("y", "d_cw", [(T.CW[0::16, :], T.BD[:])] + [(T.CW[16 * h + 2::32, :], T.cn[:]) for h in range(2)],
-                 ["BD"] + pcs("cn", 0, 4), ["CW"])
+    dmas("y", "d_cw", [(T.CW[0::16, :], T.BD[:]), (T.CW[1::16, :], T.BR[:])], ["BD", "BR"], ["CW"])
+    const_round(0)
     dmas("g", "d_q2", [(T.CD[r::4], T.x[r::4, :]) for r in (2, 3)], [], ["CDj"])
-    dmas("y", "d_j", [(T[xname(t)][t::16, 4096:5120], T.DD[0:32, :]) for t in range(RO - 2)], ["zero"], [("X0", "j"), ("X1", "j")])
-    fill(T.KL[:], 0.0, "KL")
-    fill(T.TL[:], 0.0, "TL")
-    fill(T.TR[:], 0.0, "TR")
-    fill(T.SEL[:], 0.0, "SEL")
-    fill(T.rst[:], 0.0, "rst")
-    fill(T.KR[:], 2.0 ** 21, "KR")
     fill(T.UL[:, :, 8::9], 0.0, "UL")
-    for r in (0, 64):
-        fill(T.TL[r:r + 1], 1.0, "TL")
-    fill(T.TR[96:97], 1.0, "TR")
-    fill(T.KL[64:65], 0.5, "KL")
-    fill(T.SEL[:, :, 0:144:16], -4096.0, "SEL")
-    for p in range(4):
-        fill(T.SEL[:, p, 2 ** p:144:16], -4096.0, "SEL")
-    fill(T.rst[:, :, 0::4], BIG, "rst")
-    fill(T.rst[:, 1, 1::2], 512.0, "rst")
-    fill(T.rst[:, 1, 2::4], -512.0, "rst")
-    iota(T.TL[96:97], [[0, 32], [1, 16]], 0, 0, [], ["TL"])
-    iota(T.TR[0:1, 0:9], [[0, 288], [1280, 4]], 0, 0, [], ["TR"])
-    const_low(0)
-    op("v", lambda: V.tensor_scalar(T.pc[:, 1:2], T.pc[:, 0:1], 3, None, A.bitwise_and), ["pc"], ["pc1"])
-    op("v", lambda: V.tensor_scalar(T.pc[:, 2:3], T.pc[:, 0:1], 12, None, A.bitwise_and), ["pc"], ["pc2"])
-    op("v", lambda: V.tensor_scalar(T.pf[:, 1:2], T.pc[:, 1:2], 1024.0, None, A.mult), ["pc1"], ["pf1"])
-    op("v", lambda: V.tensor_scalar(T.pf[:, 2:3], T.pc[:, 2:3], 4.0, None, A.mult), ["pc2"], ["pf2"])
-    op("v", lambda: V.tensor_scalar(T.EC[:], T.ED[:], T.pf[:, 1:2], T.pf[:, 2:3], A.add, A.add), ["ED", "pf1", "pf2"], ["EC"])
-    turned(1)
-    dmas("y", "d_cw", [(T.CW[1::16, :], T.BR[:])], ["BR"], ["CW"])
+    fill(T.SEL[:, :, 0:144:16], -4096.0, "SEL", ["SELz"])
+    fill(T.rs0[:], 0.0, "rs0")
+    const_round_v(0)
+    fill(T.rs0[:, 0::4], BIG, "rs0")
+
+    def own_values():
+        op("v", lambda: V.tensor_scalar(T.pc[:, 1:2], T.pc[:, 0:1], 3, None, A.bitwise_and), ["pc"], ["pc1"])
+        op("v", lambda: V.tensor_scalar(T.pc[:, 2:3], T.pc[:, 0:1], 12, None, A.bitwise_and), ["pc"], ["pc2"])
+        op("v", lambda: V.tensor_scalar(T.pf[:, 1:2], T.pc[:, 1:2], 1024.0, None, A.mult), ["pc1"], ["pf1"])
+        op("v", lambda: V.tensor_scalar(T.pf[:, 2:3], T.pc[:, 2:3], 4.0, None, A.mult), ["pc2"], ["pf2"])
+        op("v", lambda: V.tensor_scalar(T.EC[:], T.ED[:], T.pf[:, 1:2], T.pf[:, 2:3], A.add, A.add), ["ED", "pf1", "pf2"], ["EC"])
+        turned(1, table, ["EC"])
+        dmas("y", "d_j", [(T[xname(t)][t::16, 4096:5120], T.DD[0:32, :]) for t in range(RO - 2)], ["zero"], [("X0", "j"), ("X1", "j")])
 
     def first_maps():
         for k in range(8):
             gather("vs"[k % 2], T.W[:, 512 * k:512 * k + 512], T.CW[:], T.LA[:, 32 * k:32 * k + 32],
                    ["CW", ("LA", k // 2)], [("W", k), ("F", k // 2)], add=-128.0)
-        extract("W", 1, "EC")
-        turned(0)
+        turned(0, lambda j: T.W[1::16, 1024 * j:1024 * j + 1024], pcs("W"))
 
-    order = [(0, 0), (0, 1), (1, 0), (1, 1), (0, 2), (1, 2), (2, 0), (2, 1), (2, 2), (0, 3), (1, 3), (2, 3), (3, 0), (3, 1), (3, 2), (3, 3)]
+    def last_list():
+        for y in range(4):
+            for j in range(4):
+                mm(T.pR[:, 0, :, :, :, y], T.PB[:, y, 3 - j:131 - j], T.DG[:, 64 * j:64 * j + 64], j == 0, j == 3,
+                   pcs("DG", 0, 4) + [("PB", y), "PB"], "pR")
+
+    def g_list(t):
+        if t == RO - 1:
+            for z in range(4):
+                copy(T.LG[:, 64 * z:64 * z + 64], T.pR[:, 0, :, z], ["pR"], [("LG", z)])
+        elif t > 0:
+            copy(T.LG[:], T.DG[:], pcs("DG", 0, 4), pcs("LG", 0, 4))
+
+    by_pairs = [(j, jj) for a, b in ((0, 0), (2, 0), (0, 2), (2, 2)) for j in (a, a + 1) for jj in (b, b + 1)]
+    by_places = sorted(((j, jj) for j in range(4) for jj in range(4)), key=lambda e: (max(2 * e[0] + 1, 2 * e[1]), e))
     for t in range(RO):
         first, last = t == 0, t == RO - 1
         cs = [(k, u) for k in range(4) for u in range(4)]
@@ -438,35 +487,59 @@ def rank_program(g, core, T, topo):
         def carried():
             if not first:
                 strip_v()
-                turned(0)
+                turned(0, table, ["EC"])
 
-        if not first:
-            extract(xname(t), 15 if last else t - 1, "ED")
-        if POS[t] <= 4:
-            narrow_low("v", t, 0, 0, range(8))
-            narrow_low("s", t, 0, 1, range(8))
-            if first:
-                first_maps()
-            narrow_low("s", t, 1, 0, range(8))
+        def features(k0, k1):
             if not first:
-                strip_s()
-            narrow_low("s", t, 1, 1, range(8))
+                for k in range(k0, k1):
+                    b_piece("s", t - 1, 2 * k + 1)
+                    b_piece("v", t - 1, 2 * k)
+                if k1 == 4:
+                    dmas("y", "d_cw", [(T.CW[0::16, :], T["IR%d" % (t - 1)][:])], [("IR", t - 1)], ["CW"])
+                    extract(xname(t), 15 if last else t - 1)
+
+        if POS[t] < 4:
+            features(0, 4)
+            narrow_low("v", t, 0, 0)
+            narrow_low("s", t, 1, 0)
+            narrow_low("s", t, 0, 1)
             if first:
+                own_values()
+                narrow_low("v", t, 1, 1)
+                first_maps()
                 dmas("g", "d_ac", [(T.X0[15::16, 0:4096], T.W[2::16, 0:4096])], pcs("W"), pcs("X0"), accum_op=A.add, max_dma_last_dim=4096)
-            for j in range(4):
-                scan_low(t, 0, j)
-                if j == 2:
+            else:
+                strip_s()
+                narrow_low("s", t, 1, 1)
+            for i, (j, jj) in enumerate(by_pairs):
+                scan_low(t, i, j, jj)
+                if i == 3:
+                    g_list(t)
+                if i == 5:
                     carried()
-            c_some("s", 12)
-            for j in range(4):
-                scan_low(t, 1, j)
-                if j == 1 and POS[t] < 4:
-                    offsets_low(t, 0)
-            c_list(0)
-            offsets_low(t, 1)
+            c_some("s", NS)
+            offsets_low()
+        elif POS[t] == 4:
+            features(0, 4)
+            narrow_mid("v", t, 0, 0)
+            narrow_mid("s", t, 0, 1)
+            narrow_mid("s", t, 1, 0)
+            strip_s()
+            narrow_mid("s", t, 1, 1)
+            for h in range(2):
+                for j in range(4):
+                    scan_mid(h, j)
+                    if (h, j) == (0, 1):
+                        g_list(t)
+                    if (h, j) == (0, 2):
+                        carried()
+            c_some("s", NS)
+            offsets_mid()
         else:
-            narrow_high("v", t, 0, 0)
+            features(0, 1)
             narrow_high("s", t, 1, 0)
+            narrow_high("v", t, 0, 0)
+            features(1, 4)
             narrow_high("s", t, 1, 1)
             narrow_high("v", t, 0, 1)
             narrow_high("s", t, 1, 2)
@@ -474,55 +547,46 @@ def rank_program(g, core, T, topo):
             strip_s()
             narrow_high("s", t, 1, 3)
             narrow_high("s", t, 0, 3)
-            for i, (j, jj) in enumerate(order):
+            for i, (j, jj) in enumerate(by_places):
                 scan_high(i, j, jj)
+                if i == 3:
+                    g_list(t)
                 if i == 6:
                     carried()
-            c_some("s", 12)
-            c_list(0)
+            c_some("s", NS)
             offsets_high(t)
         for u in range(4):
             select("vs"[u % 2], t, u)
         spread(t)
-        c_some("v", 2)
-        c_some("s", 2)
+        for i in range(16 - NS):
+            c_some("vs"[i % 2], 1)
         c_dense(3)
-        c_list(1)
+        c_list(0, 2)
         for k in range(4):
-            if k >= 2:
-                c_list(k)
-            a_piece("v", 2 * k)
-            a_piece("s", 2 * k + 1)
+            a_piece("v", k, 0, AV[k])
+            a_piece("s", k, AV[k], 64)
             a_dense("DD", "d_d%d" % k, 0, k, k + 1)
+            if k == 0:
+                c_list(2, 4)
             if k == 2:
                 d_send(t, 0)
-        for k in range(1, 4):
-            d_send(t, k)
+        d_send(t, 1)
         if last:
+            d_send(t, 2)
+            d_send(t, 3)
             break
         di = "DI%d" % (t % 2)
         dmas("y", "d_i", [(T[di][:], T.AO[1::16, :])], pcs("AO"), [di])
-        send("n%d" % t, T["IR%d" % t][:], T[di][:], [di], [("IR", t)], 1, "d_l2")
         a_dense("DG", "d_g0", 2, 0, 4)
-        if t < 3:
-            const_low(t + 1)
+        const_round_v(t + 1)
+        d_send(t, 2)
+        d_send(t, 3)
+        send("n%d" % t, T["IR%d" % t][:], T[di][:], [di], [("IR", t)], 1, "d_l2")
+        const_round(t + 1)
         if t == 3:
             const_high()
-        if t == 4:
-            const_high_v()
-        if t < RO - 2:
-            copy(T.LG[:], T.DG[:], pcs("DG", 0, 4), pcs("LG", 0, 4))
-        else:
-            for y in range(4):
-                for j in range(4):
-                    mm(T.pR[:, 0, :, :, :, y], T.PB[:, y, 3 - j:131 - j], T.DG[:, 64 * j:64 * j + 64], j == 0, j == 3,
-                       pcs("DG", 0, 4) + [("PB", y), "PB"], "pR")
-        for k in range(8):
-            b_piece("vs"[k % 2], t, k)
-            if k == 4 and t == RO - 2:
-                for z in range(4):
-                    copy(T.LG[:, 64 * z:64 * z + 64], T.pR[:, 0, :, z], ["pR"], [("LG", z)])
-        dmas("y", "d_cw", [(T.CW[0::16, :], T["IR%d" % t][:])], [("IR", t)], ["CW"])
+        if t == RO - 2:
+            last_list()
 
     for k in range(4):
         dmas("y", "d_out", [(T.yo[:, 64 * k:64 * k + 64], T.YR[:, 64 * k:64 * k + 64])], [("YR", k)], [])

from concourse.mybir import dt, AluOpType, AxisListType, ActivationFunctionType

RO = 8
POS = [0, 1, 2, 3, 4, 7, 8, 9]
BIG = 2.0 ** 40
NS = 10
AV = [32, 26, 32, 26]

SCRATCH = {
    "X0": ("sbuf", [128, 5120], "float32"),
    "X1": ("sbuf", [128, 5120], "float32"),
    "W": ("sbuf", [128, 5120], "float32"),
    "AO": ("sbuf", [128, 4096], "float32"),
    "CW": ("sbuf", [128, 4096], "float32"),
    "CO": ("sbuf", [128, 4096], "float32"),
    "CD": ("sbuf", [128, 4, 1024], "float32"),
    "TH": ("sbuf", [128, 1024], "float32"),
    "xb": ("sbuf", [128, 4096], "bfloat16"),
    "UL": ("sbuf", [128, 4, 1152], "bfloat16"),
    "ML": ("sbuf", [128, 2, 1152, 4], "bfloat16"),
    "UH": ("sbuf", [128, 8, 640], "bfloat16"),
    "MH": ("sbuf", [128, 4, 640], "bfloat16"),
    "oi": ("sbuf", [128, 256], "int32"),
    "LN": ("sbuf", [128, 256], "uint16"),
    "LA": ("sbuf", [128, 256], "uint16"),
    "LR": ("sbuf", [128, 256], "uint16"),
    "LC": ("sbuf", [128, 256], "uint16"),
    "LG": ("sbuf", [128, 256], "uint16"),
    "LS": ("sbuf", [128, 64], "uint16"),
    "OF": ("sbuf", [128, 8, 4, 2, 4], "float32"),
    "ED": ("sbuf", [128, 256], "float32"),
    "EH": ("sbuf", [128, 256], "bfloat16"),
    "EC": ("sbuf", [128, 256], "float32"),
    "DD": ("sbuf", [128, 256], "float32"),
    "DG": ("sbuf", [128, 256], "float32"),
    "DC": ("sbuf", [128, 256], "float32"),
    "BD": ("sbuf", [128, 256], "float32"),
    "BR": ("sbuf", [128, 256], "float32"),
    "YR": ("sbuf", [128, 256], "float32"),
    "cn": ("sbuf", [128, 128], "float32"),
    "one": ("sbuf", [128, 128], "float32"),
    "SEL": ("sbuf", [128, 5, 144], "bfloat16"),
    "KL": ("sbuf", [128, 128], "bfloat16"),
    "KR": ("sbuf", [128, 256], "bfloat16"),
    "TL": ("sbuf", [128, 128], "bfloat16"),
    "TR": ("sbuf", [128, 256], "bfloat16"),
    "rs0": ("sbuf", [128, 256], "float32"),
    "rs1": ("sbuf", [128, 128], "float32"),
    "SL": ("sbuf", [128, 256], "int32"),
    "SA": ("sbuf", [128, 64], "int32"),
    "RI": ("sbuf", [128, 2, 2, 2, 8], "int32"),
    "RB": ("sbuf", [128, 64], "bfloat16"),
    "idn": ("sbuf", [128, 128], "bfloat16"),
    "MS": ("sbuf", [128, 128], "bfloat16"),
    "m16": ("sbuf", [128, 8], "bfloat16"),
    "S16": ("sbuf", [128, 128], "bfloat16"),
    "tmp": ("sbuf", [128, 128], "int32"),
    "pc": ("sbuf", [128, 4], "int32"),
    "pf": ("sbuf", [128, 4], "float32"),
    "PA": ("sbuf", [128, 4, 144], "float32"),
    "PB": ("sbuf", [128, 4, 132], "float32"),
    "pK0": ("psum", [128, 512], "float32"),
    "pL": ("psum", [128, 8, 64], "float32"),
    "pR": ("psum", [128, 2, 8, 4, 2, 4], "float32"),
    "pS": ("psum", [128, 512], "float32"),
}
for _t in range(RO - 1):
    SCRATCH["DS%d" % _t] = ("sbuf", [128, 256], "uint16")
    SCRATCH["DI%d" % (_t % 2)] = ("sbuf", [128, 256], "float32")
    SCRATCH["LD%d" % _t] = ("sbuf", [128, 256], "uint16")
    SCRATCH["IR%d" % _t] = ("sbuf", [128, 256], "float32")

SEMAPHORES = ["v", "s", "p", "gc", "d_ls", "d_l2", "d_o", "d_x", "d_z", "d_q1", "d_q2", "d_g0", "d_j", "d_b", "d_cw", "d_ex", "d_cd",
              "d_w", "d_ac", "d_i", "d_out", "ra", "rb"]
SEMAPHORES += ["d_%s%d" % (_n, _k) for _n in "dc" for _k in range(4)]
SEMAPHORES += ["m%d_%d" % (_t, _k) for _t in range(RO) for _k in range(4)]
SEMAPHORES += ["n%d" % _t for _t in range(RO - 1)]


def rank_program(g, core, T, topo):
    rank = T.rank_of(core)
    if rank is None:
        return
    A = AluOpType
    AF = ActivationFunctionType
    V, S, P = g.vector, g.scalar, g.tensor
    n = len(T.cores)

    queues = {"v": V, "s": S, "p": P, "y": g.sync, "g": g}
    total = {}
    waited = {q: {} for q in queues}
    writer = {}
    readers = {}

    def need(q, reads, writes):
        toks = []
        for k in reads:
            if k in writer:
                toks.append(writer[k])
        for k in writes:
            if k in writer:
                toks.append(writer[k])
            toks.extend(readers.get(k, {}).items())
        best = {}
        for sem, cnt in toks:
            if q == "p" and sem == "p":
                continue
            if sem.startswith("d_"):
                cnt = total[sem]
            best[sem] = max(best.get(sem, 0), cnt)
        for sem, cnt in best.items():
            if waited[q].get(sem, 0) < cnt:
                queues[q].wait_ge(T.sem[sem], cnt)
                waited[q][sem] = cnt

    def done(tok, reads, writes):
        for k in reads:
            readers.setdefault(k, {})[tok[0]] = tok[1]
        for k in writes:
            writer[k] = tok
            readers[k] = {}

    def op(q, fn, reads, writes):
        if q == "g":
            writes = writes + ["pool"]
        need(q, reads, writes)
        sem = "gc" if q == "g" else q
        fn().then_inc(T.sem[sem], 1)
        total[sem] = total.get(sem, 0) + 1
        done((sem, total[sem]), reads, writes)

    def dmas(q, sem, pairs, reads, writes, **kw):
        need(q, reads, writes)
        for o_, i_ in pairs:
            queues[q].dma_start(o_, i_, **kw).then_inc(T.sem[sem], 16)
            total[sem] = total.get(sem, 0) + 16
        done((sem, total[sem]), reads, writes)

    def send(sem, o_, i_, reads, landed, hop=1, left="d_ls"):
        dst, src = T.cores[(rank + hop) % n], T.cores[(rank - hop) % n]
        rid, pid, _se = topo.addr(dst)
        need("g", reads, [])
        g.remote_dma(o_, i_, T.sem[sem], T.sem[left], pid, rid, topo.mask(core, dst))
        total[left] = total.get(left, 0) + len(topo.engines(core, dst))
        done((left, total[left]), reads, [])
        total[sem] = len(topo.engines(src, core))
        for k in landed:
            writer[k] = (sem, total[sem])

    def pcs(name, a=0, b=8):
        return [(name, k) for k in range(a, b)]

    def gather(q, o_, win, lst, reads, writes, scale=None, add=None):
        i_ = win.indirect(lst)
        if q == "s":
            fn = lambda: S.activation(o_, i_, AF.Identity, bias=(add or 0.0), scale=(scale or 1.0))
        elif scale is not None:
            fn = lambda: V.tensor_scalar(o_, i_, scale, None, A.mult)
        elif add is not None:
            fn = lambda: V.tensor_scalar(o_, i_, add, None, A.add)
        else:
            fn = lambda: V.tensor_copy(o_, i_)
        op(q, fn, reads, writes)

    def copy(o_, i_, reads, writes):
        op("v", lambda: V.tensor_copy(o_, i_), reads, writes)

    def fill(ap, val, key, after=()):
        op("v", lambda: V.memset(ap, val), list(after), [key])

    def iota(ap, pattern, base, cm, reads, writes):
        op("g", lambda: g.iota(ap, pattern, base, cm, allow_small_or_imprecise_dtypes=True), reads, writes)

    def mm(o_, l_, r_, start, stop, reads, bank):
        op("p", lambda: P.matmul(o_, l_, r_, start, stop), reads, [bank])

    def xname(t):
        return "X%d" % (t % 2)

    def a_piece(q, k, c0, c1):
        gather(q, T.AO[:, 1024 * k + 16 * c0:1024 * k + 16 * c1], T.W[:, 0:4096], T.LC[:, 64 * k + c0:64 * k + c1], ["W", ("LC", k)],
               [("AO", 2 * k + (c0 > 0))])

    def b_piece(q, t, k):
        x, y = xname(t), xname(t + 1)
        gather(q, T[y][:, 512 * k:512 * k + 512], T[x][:, 0:4096], T["LD%d" % t][:, 32 * k:32 * k + 32],
               pcs(x) + [("LD", t, k // 2)], [(y, k)])

    def c_piece(q, lst, k, u, add=None):
        c0 = 64 * k + 16 * u
        gather(q, T.CO[:, 1024 * k + u:1024 * k + 1024:4], T.CW[:], T[lst][:, c0:c0 + 16], ["CW", (lst, k)], [("CO", k, u)], add=add)

    def c_dense(k):
        dmas("y", "d_c%d" % k, [(T.DC[:, 64 * k:64 * k + 64], T.CO[0::16, 1024 * k:1024 * k + 1024])],
             [("CO", k, u) for u in range(4)], [("DC", k)])

    def c_list(k0, k1):
        copy(T.LC[:, 64 * k0:64 * k1], T.DC[:, 64 * k0:64 * k1], pcs("DC", k0, k1), pcs("LC", k0, k1))

    def a_dense(name, sem, row, k0, k1):
        dmas("y", sem, [(T[name][:, 64 * k:64 * k + 64], T.AO[row::16, 1024 * k:1024 * k + 1024]) for k in range(k0, k1)],
             pcs("AO", 2 * k0, 2 * k1), [(name, k) for k in range(k0, k1)] + ["zero"] * (name == "DD" and k0 == 0))

    def d_send(t, k):
        ds = "DS%d" % t
        cols = slice(64 * k, 64 * k + 64)
        if t == RO - 1:
            send("m%d_%d" % (t, k), T.YR[:, cols], T.DD[:, cols], [("DD", k)], [("YR", k)])
            return
        copy(T[ds][:, cols], T.DD[:, cols], [("DD", k)], [(ds, k)])
        send("m%d_%d" % (t, k), T["LD%d" % t][:, cols], T[ds][:, cols], [(ds, k)], [("LD", t, k)])

    def extract(name, row):
        dmas("y", "d_ex", [(T.ED[j::4, :], T[name][row::16, 1024 * j:1024 * j + 1024]) for j in range(4)], pcs(name), ["ED"])

    def strip_s():
        op("s", lambda: S.activation(T.EH[:], T.ED[:], AF.Identity, bias=128.0, scale=2.0 ** -14), ["ED"], ["EH"])
        op("s", lambda: S.activation(T.pS[:, 0:256], T.EH[:], AF.Identity, bias=2.0 ** 21, scale=-16384.0), ["EH"], ["pS"])

    def strip_v():
        op("v", lambda: V.tensor_tensor(T.EC[:], T.ED[:], T.pS[:, 0:256], A.add), ["ED", "pS"], ["EC"])

    def table(j):
        return T.EC[j::4, :]

    def turned(row, src, keys):
        dmas("y", "d_cd", [(T.CD[4 * j + row::16, :, 256 * r:256 * r + 256], src((j + r) % 4))
                           for r in range(4) for j in range(4)], keys, [("CD", row)])

    def select(q, t, u):
        far = u ^ (2 ** (POS[t] - 8)) if POS[t] >= 8 else u
        gather(q, T.TH[:, 256 * u:256 * u + 256], T.CD[:, far, :], T.LS[:, 16 * u:16 * u + 16],
               [("CD", 0), ("CD", 1), "CDj", "LS0", "LS1"], [("TH", u)])

    def spread(t):
        th = pcs("TH", 0, 4)
        pairs = [(T.W[0::16, 0:4096], T.TH[0::4, :])]
        if t < RO - 1:
            pairs += [(T.W[2::16, 0:4096], T.TH[1::4, :]), (T.W[1::16, 1024:5120], T.TH[0::4, :]), (T.W[1::16, 0:1024], T.TH[12::16, :])]
        dmas("y", "d_w", pairs, th, ["W"] + pcs("W"))
        if t < RO - 2:
            x = xname(t)
            dmas("g", "d_ac", [(T[x][t::16, 1024:5120], T.TH[0::4, :]), (T[x][t::16, 0:1024], T.TH[12::16, :])],
                 th + [(x, "j")], pcs(x), accum_op=A.add, max_dma_last_dim=4096)

    def narrow(q, o_, i_, m, reads, writes):
        if q == "v":
            op(q, lambda: V.tensor_scalar(o_, i_, 2.0 ** -14, 128.0 + 16 * m, A.mult, A.add), reads, writes)
        else:
            op(q, lambda: S.activation(o_, i_, AF.Identity, bias=128.0 + 16 * m, scale=2.0 ** -14), reads, writes)

    def around(p, b, m):
        return ((m >> p) << (p + 1)) + (b << p) + (m & (2 ** p - 1))

    ties = ["TL", "TR", "TL32", "TR0", "TR32", "TR64"]

    def open_keys(wd):
        mm(T.pK0[:, 0:wd], T.KL[:], T.KR[:, 0:wd], True, False, ["KL", "KL0", "KL32", "KR"], "pK0")

    def close_keys(wd):
        mm(T.pK0[:, 0:wd], T.TL[:], T.TR[:, 0:wd], False, True, ties, "pK0")

    def least(rs, c0, wd):
        op("v", lambda: V.tensor_tensor_scan(T.SL[:, c0:c0 + wd], T[rs][:, 0:wd], T.pK0[:, 0:wd], 0.0, A.add, A.min), [rs, "pK0"], [("SL", c0)])

    def narrow_low(q, t, b, jp):
        x = xname(t)
        for m in range(8):
            c0 = 2048 * jp + around(POS[t], b, m)
            narrow(q, T.UL[:, 2 * jp + b, m::9], T[x][:, c0:2048 * jp + 2048:16], m, pcs(x, 4 * jp, 4 * jp + 4) + ["UL"], [("UL", jp, b, m)])

    def scan_low(t, i, j, jj):
        p = POS[t]
        s = (jj - j) % 4
        side = lambda b, y: T.UL[:, 2 * (y // 2) + b, 576 * (y % 2):576 * (y % 2) + 576]
        if i == 0:
            open_keys(256)
        op("v", lambda: V.tensor_tensor_scan(T.MH[:, i % 4, 0:576], side(0, j), side(1, jj), 0.0, A.max, A.min),
           [("UL", y // 2, b, m) for b, y in ((0, j), (1, jj)) for m in range(8)], [("MH", i % 4)])
        for m in range(8):
            c0 = around(p, 0, m)
            mm(T.pK0[:, s:256:4], T.SEL[:, p, 16 - c0:144 - c0], T.MH[:, i % 4, m:576:9], False, False, [("MH", i % 4), "SEL", ("SEL", p)], "pK0")
        if i == 15:
            close_keys(256)

    def offsets_low():
        least("rs0", 0, 256)
        op("v", lambda: V.tensor_scalar(T.SA[:], T.SL[:, 3::4], 1023, None, A.bitwise_and), [("SL", 0)], ["SA"])
        copy(T.LS[:], T.SA[:], ["SA"], ["LS0", "LS1"])

    def narrow_mid(q, t, h, b):
        x = xname(t)
        for m in range(8):
            narrow(q, T.UL[:, 2 * h + b, m::9], T[x][:, 16 * b + 8 * h + m:4096:32], m, pcs(x) + ["UL"], [("UL", h, b, m)])

    def scan_mid(h, j):
        rd = [("UL", h, b, m) for b in range(2) for m in range(8)]
        if j == 0 and h == 0:
            open_keys(128)
        for s in range(4):
            jj = (j + s) % 4
            op("v", lambda: V.tensor_tensor_scan(T.ML[:, h, 288 * j:288 * j + 288, s], T.UL[:, 2 * h, 288 * j:288 * j + 288],
                                                 T.UL[:, 2 * h + 1, 288 * jj:288 * jj + 288], 0.0, A.max, A.min), rd, [("ML", h, j, s)])
        for m in range(8):
            c0 = 8 * h + m
            mm(T.pK0[:, 0:128], T.SEL[:, 4, 16 - c0:144 - c0], T.ML[:, h, 288 * j + m:288 * j + 288:9, :], False, False,
               [("ML", h, j, s) for s in range(4)] + ["SEL"], "pK0")
        if j == 3 and h == 1:
            close_keys(128)

    def offsets_mid():
        least("rs1", 128, 128)
        least("rs0", 0, 128)
        op("v", lambda: V.tensor_scalar(T.SL[:, 131::4], T.SL[:, 131::4], -272.0, None, A.add), [("SL", 128)], [("SL", 128)])
        op("v", lambda: V.tensor_scalar(T.SA[:], T.SL[:, 3::4], 1023, None, A.bitwise_and), [("SL", 0), ("SL", 128)], ["SA"])
        for b in range(2):
            copy(T.LS[:, b::2], T.SA[:, 32 * b:32 * b + 32], ["SA"], ["LS%d" % b])

    def narrow_high(q, t, b, j):
        x = xname(t)
        for m in range(4):
            c0 = 1024 * j + 128 * around(POS[t] - 7, b, m)
            narrow(q, T.UH[:, 4 * b + j, m::5], T[x][:, c0:c0 + 128], m, pcs(x, 2 * j, 2 * j + 2) + ["UH"], [("UH", b, j, m)])

    def scan_high(i, j, jj):
        s = (jj - j) % 4
        if i == 0:
            mm(T.pK0[:, 0:128], T.idn[:], T.MS[:], True, False, ["idn", "MS"], "pK0")
        op("v", lambda: V.tensor_tensor_scan(T.MH[:, i % 4], T.UH[:, j], T.UH[:, 4 + jj], 0.0, A.max, A.min),
           [("UH", b, y, m) for b, y in ((0, j), (1, jj)) for m in range(4)], [("MH", i % 4)])
        for m in range(4):
            mm(T.pK0[:, 32 * m + s:32 * m + 32:4], T.MH[:, i % 4, m::5], T.m16[:], False, i == 15 and m == 3, [("MH", i % 4), "m16"], "pK0")

    def offsets_high(t):
        e = POS[t] - 7
        side = lambda b: [T.RI[:, :, :, b, :], T.RI[:, :, b, :, :], T.RI[:, b, :, :, :]][e]
        mm(T.pL[:, 0], T.TL[:], T.TR[:, 0:64], True, False, ties, "pL")
        least("rs0", 0, 128)
        op("v", lambda: V.tensor_scalar(side(0), T.SL[:, 3:128:4], 2, 3, A.logical_shift_right, A.bitwise_and), [("SL", 0)], ["RI0"])
        op("v", lambda: V.tensor_scalar(side(1), T.SL[:, 3:128:4], 3, None, A.bitwise_and), [("SL", 0)], ["RI1"])
        copy(T.RB[:], T.RI[:], ["RI0", "RI1"], ["RB"])
        mm(T.pL[:, 0], T.S16[:], T.RB[:], False, True, ["S16", "RB"], "pL")
        copy(T.LS[:], T.pL[:, 0], ["pL"], ["LS0", "LS1"])

    def const_round(t):
        p = POS[t]
        if p < 4:
            iota(T.KL[0:1], [[0, 128 // 2 ** p], [16, 2 ** p]], 135, 0, ["KL"], ["KL0"])
            iota(T.KL[32:33], [[0, 8], [16 * 2 ** p, 8 // 2 ** p], [0, 2 ** (p + 1)]], 0, 0, ["KL"], ["KL32"])
            iota(T.TL[32:33], [[0, 64 // 2 ** p], [1, 2], [0, 2 ** p]], 0, 0, ["TL"], ["TL32"])
            iota(T.TR[32:33], [[0, 128], [-512, 2]], 256 - 2 ** (p + 1), 0, ["TR"], ["TR32"])
            iota(T.TR[64:65], [[0, 4], [16, 16], [0, 4]], 2 ** p, 0, ["TR"], ["TR64"])
        elif p == 4:
            iota(T.TR[32:33, 0:128], [[0, 128]], 0, 0, ["TR"], ["TR32"])
            iota(T.TR[64:65, 0:128], [[0, 4], [32, 8], [0, 4]], 16, 0, ["TR"], ["TR64"])
        elif p == 7:
            iota(T.TR[0:1, 0:64], [[0, 64]], 0, 0, ["TR"], ["TR0"])
            iota(T.TR[64:65, 0:64], [[0, 4], [-128, 2], [16, 8]], 128, 0, ["TR"], ["TR64"])
        elif p == 8:
            iota(T.TR[64:65, 0:64], [[0, 4], [128, 2], [16, 8]], 0, 0, ["TR"], ["TR64"])

    def const_round_v(t):
        if POS[t] < 4:
            fill(T.SEL[:, POS[t], 2 ** POS[t]:144:16], -4096.0, ("SEL", POS[t]), ["SEL"])
        if POS[t] == 3:
            fill(T.rs1[:], 512.0, "rs1")
            fill(T.rs1[:, 0::4], BIG, "rs1")
            fill(T.rs1[:, 2::4], -512.0, "rs1")
        if POS[t] == 4:
            fill(T.m16[:], -16.0, "m16")
            fill(T.UH[:, :, 4::5], 0.0, "UH")
            fill(T.PB[:, :, 0:3], 0.0, "PB")
        if POS[t] == 7:
            op("v", lambda: V.tensor_scalar(T.tmp[:], T.tmp[:], 15, None, A.bitwise_and), ["tmp"], ["tmp"])
            op("v", lambda: V.tensor_scalar(T.S16[:], T.tmp[:], 0.0, 256.0, A.is_equal, A.mult), ["tmp"], ["S16"])

    def const_high():
        op("g", lambda: g.affine_select(T.idn[:], T.one[:], [[-1, 128]], A.is_equal, 0.0, 0, 1), ["one"], ["idn"])
        iota(T.MS[:], [[0, 32], [10, 2], [3, 2]], 1, 0, [], ["MS"])
        op("g", lambda: g.affine_select(T.MS[:], T.MS[:], [[0, 4], [-16, 8], [0, 4]], A.is_ge, 0.0, 0, 1), ["MS"], ["MS"])
        op("g", lambda: g.affine_select(T.MS[:], T.MS[:], [[0, 4], [16, 8], [0, 4]], A.is_ge, 0.0, 15, -1), ["MS"], ["MS"])
        op("g", lambda: g.iota(T.tmp[:], [[0, 8], [-1, 16]], 16, 1), [], ["tmp"])
        for y in range(4):
            op("g", lambda: g.affine_select(T.PB[:, y, 3:131], T.one[:], [[-16, 8], [-1, 4], [-1000, 4]], A.is_equal, 0.0, -4 * y, 1),
               ["one", "PB"], [("PB", y)])

    dmas("y", "d_o", [(T.oi[:], T.o[:])], [], ["oi"])
    fill(T.DD[:], 0.0, "zero")
    fill(T.one[:], 1.0, "one")
    dmas("y", "d_z", [(T.AO[0::16, :], T.DD[:]), (T.X1[0::16, 0:4096], T.DD[:])], ["zero"], ["AOz", "X1z"])
    dmas("y", "d_x", [(T.xb[:, 0:2048], T.x[:, 0:2048])], [], ["xb"])
    dmas("s", "d_x", [(T.xb[:, 2048:4096], T.x[:, 2048:4096])], [], ["xb2"])
    fill(T.PA[:, :, 0:12], 0.0, "PA")
    fill(T.KL[:], 0.0, "KLz")
    fill(T.TL[:], 0.0, "TLz")
    fill(T.TR[:], 0.0, "TRz")
    fill(T.SEL[:], 0.0, "SELz")
    fill(T.KR[:], 2.0 ** 21, "KR")
    fill(T.KL[64:65], 0.5, "KL", ["KLz"])
    fill(T.TL[0:1], 1.0, "TL0", ["TLz"])
    fill(T.TL[64:65], 1.0, "TL64", ["TLz"])
    fill(T.TR[96:97], 1.0, "TR", ["TRz"])
    for z in range(2):
        iota(T.W[:, 1024 * z:1024 * z + 1024], [[128, 8], [1, 32], [1024, 4]], 128 + 32 * z, 0, [], [("F", z)])
        if z == 0:
            dmas("g", "d_q1", [(T.CW[:], T.x[:])], [], ["CW"])
    for j in range(4):
        op("g", lambda: g.affine_select(T.PA[:, j, 12:140], T.one[:], [[-16, 8], [-1000, 4], [-4, 4]], A.is_equal, 0.0, -j, 1),
           ["one", "PA"], [("PA", j)])
    copy(T.LN[:], T.oi[:], ["oi"], ["LN"])
    for z in range(4):
        copy(T.OF[:, :, z], T.oi[:, 64 * z:64 * z + 64], ["oi"], [("OF", z)])
    for j in range(4):
        for y in range(4):
            mm(T.pL[:, j], T.PA[:, j, 12 - 4 * y:140 - 4 * y], T.OF[:, :, :, :, y], y == 0, y == 3, pcs("OF", 0, 4) + [("PA", j)], "pL")
    for z in range(2):
        op("s", lambda: S.activation(T.X1[:, 0:4096].indirect(T.LN[:, 64 * z:64 * z + 64]), T.W[:, 1024 * z:1024 * z + 1024], AF.Silu),
           [("F", z), "LN", "X1z"], pcs("X1"))
        op("v", lambda: V.tensor_scalar(T.AO[:].indirect(T.LN[:, 128 + 64 * z:192 + 64 * z]), T.W[:, 0:1024], 1.0, 64.0 + 32 * z,
                                        A.mult, A.add), [("F", 0), "LN", "AOz"], pcs("AO"))
    dmas("y", "d_b", [(T.DG[:], T.AO[0::16, :]), (T.DC[:], T.X1[0::16, 0:4096])], pcs("AO") + pcs("X1"), ["B1"])
    copy(T.LA[:], T.pL[:, 0:4], ["pL"], pcs("LA", 0, 4))
    for h in range(4):
        iota(T.cn[32 * h:32 * h + 32, :], [[1, 128]], 128, 128, [], [("cn", h)])
    op("g", lambda: g.iota(T.pc[:, 0:1], [[0, 1]], 0, 1), [], ["pc"])
    iota(T.ED[:], [[1, 16], [64, 16]], 0, 0, [], ["ED"])
    iota(T.TL[96:97], [[0, 8], [1, 16]], 0, 0, ["TL0", "TL64"], ["TL"])
    iota(T.TR[0:1], [[0, 64], [1280, 4]], 0, 0, ["TR"], ["TR0"])
    dmas("y", "d_cw", [(T.CW[16 * h + 2::32, :], T.cn[:]) for h in range(2)], pcs("cn", 0, 4), ["CW"])
    send("ra", T.LR[:], T.LA[:], pcs("LA", 0, 4), pcs("LR", 0, 4), -1, "d_l2")
    for k in range(8):
        gather("vsvssvss"[k], T.X0[:, 512 * k:512 * k + 512], T.xb[:], T.LA[:, 32 * k:32 * k + 32],
               ["xb", "xb2", ("LA", k // 2)], [("X0", k)], scale=16384.0)
        if k == 2:
            op("v", lambda: V.tensor_tensor(T.BD[:], T.DG[:], T.DC[:], A.add), ["B1"], ["BD"] + pcs("DG", 0, 4) + pcs("DC", 0, 4))
            send("rb", T.BR[:], T.BD[:], ["BD"], ["BR"], -1, "d_l2")
    dmas("y", "d_cw", [(T.CW[0::16, :], T.BD[:]), (T.CW[1::16, :], T.BR[:])], ["BD", "BR"], ["CW"])
    const_round(0)
    dmas("g", "d_q2", [(T.CD[r::4], T.x[r::4, :]) for r in (2, 3)], [], ["CDj"])
    fill(T.UL[:, :, 8::9], 0.0, "UL")
    fill(T.SEL[:, :, 0:144:16], -4096.0, "SEL", ["SELz"])
    fill(T.rs0[:], 0.0, "rs0")
    const_round_v(0)
    fill(T.rs0[:, 0::4], BIG, "rs0")

    def own_values():
        op("v", lambda: V.tensor_scalar(T.pc[:, 1:2], T.pc[:, 0:1], 3, None, A.bitwise_and), ["pc"], ["pc1"])
        op("v", lambda: V.tensor_scalar(T.pc[:, 2:3], T.pc[:, 0:1], 12, None, A.bitwise_and), ["pc"], ["pc2"])
        op("v", lambda: V.tensor_scalar(T.pf[:, 1:2], T.pc[:, 1:2], 1024.0, None, A.mult), ["pc1"], ["pf1"])
        op("v", lambda: V.tensor_scalar(T.pf[:, 2:3], T.pc[:, 2:3], 4.0, None, A.mult), ["pc2"], ["pf2"])
        op("v", lambda: V.tensor_scalar(T.EC[:], T.ED[:], T.pf[:, 1:2], T.pf[:, 2:3], A.add, A.add), ["ED", "pf1", "pf2"], ["EC"])
        turned(1, table, ["EC"])
        dmas("y", "d_j", [(T[xname(t)][t::16, 4096:5120], T.DD[0:32, :]) for t in range(RO - 2)], ["zero"], [("X0", "j"), ("X1", "j")])

    def first_maps():
        for k in range(8):
            gather("vs"[k % 2], T.W[:, 512 * k:512 * k + 512], T.CW[:], T.LA[:, 32 * k:32 * k + 32],
                   ["CW", ("LA", k // 2)], [("W", k), ("F", k // 2)], add=-128.0)
        turned(0, lambda j: T.W[1::16, 1024 * j:1024 * j + 1024], pcs("W"))

    def last_list():
        for y in range(4):
            for j in range(4):
                mm(T.pR[:, 0, :, :, :, y], T.PB[:, y, 3 - j:131 - j], T.DG[:, 64 * j:64 * j + 64], j == 0, j == 3,
                   pcs("DG", 0, 4) + [("PB", y), "PB"], "pR")

    def g_list(t):
        if t == RO - 1:
            for z in range(4):
                copy(T.LG[:, 64 * z:64 * z + 64], T.pR[:, 0, :, z], ["pR"], [("LG", z)])
        elif t > 0:
            copy(T.LG[:], T.DG[:], pcs("DG", 0, 4), pcs("LG", 0, 4))

    by_pairs = [(j, jj) for a, b in ((0, 0), (2, 0), (0, 2), (2, 2)) for j in (a, a + 1) for jj in (b, b + 1)]
    by_places = sorted(((j, jj) for j in range(4) for jj in range(4)), key=lambda e: (max(2 * e[0] + 1, 2 * e[1]), e))
    for t in range(RO):
        first, last = t == 0, t == RO - 1
        cs = [(k, u) for k in range(4) for u in range(4)]

        def c_some(q, cnt):
            for _ in range(cnt):
                k, u = cs.pop(0)
                c_piece(q, "LR" if first else "LG", k, u, -128.0 if first else None)
                if u == 3 and k < 3:
                    c_dense(k)

        def carried():
            if not first:
                strip_v()
                turned(0, table, ["EC"])

        def features(k0, k1):
            if not first:
                for k in range(k0, k1):
                    b_piece("s", t - 1, 2 * k + 1)
                    b_piece("v", t - 1, 2 * k)
                if k1 == 4:
                    dmas("y", "d_cw", [(T.CW[0::16, :], T["IR%d" % (t - 1)][:])], [("IR", t - 1)], ["CW"])
                    extract(xname(t), 15 if last else t - 1)

        if POS[t] < 4:
            features(0, 4)
            narrow_low("v", t, 0, 0)
            narrow_low("s", t, 1, 0)
            narrow_low("s", t, 0, 1)
            if first:
                own_values()
                narrow_low("v", t, 1, 1)
                first_maps()
                dmas("g", "d_ac", [(T.X0[15::16, 0:4096], T.W[2::16, 0:4096])], pcs("W"), pcs("X0"), accum_op=A.add, max_dma_last_dim=4096)
            else:
                strip_s()
                narrow_low("s", t, 1, 1)
            for i, (j, jj) in enumerate(by_pairs):
                scan_low(t, i, j, jj)
                if i == 3:
                    g_list(t)
                if i == 5:
                    carried()
            c_some("s", NS)
            offsets_low()
        elif POS[t] == 4:
            features(0, 4)
            narrow_mid("v", t, 0, 0)
            narrow_mid("s", t, 0, 1)
            narrow_mid("s", t, 1, 0)
            strip_s()
            narrow_mid("s", t, 1, 1)
            for h in range(2):
                for j in range(4):
                    scan_mid(h, j)
                    if (h, j) == (0, 1):
                        g_list(t)
                    if (h, j) == (0, 2):
                        carried()
            c_some("s", NS)
            offsets_mid()
        else:
            features(0, 1)
            narrow_high("s", t, 1, 0)
            narrow_high("v", t, 0, 0)
            features(1, 4)
            narrow_high("s", t, 1, 1)
            narrow_high("v", t, 0, 1)
            narrow_high("s", t, 1, 2)
            narrow_high("s", t, 0, 2)
            strip_s()
            narrow_high("s", t, 1, 3)
            narrow_high("s", t, 0, 3)
            for i, (j, jj) in enumerate(by_places):
                scan_high(i, j, jj)
                if i == 3:
                    g_list(t)
                if i == 6:
                    carried()
            c_some("s", NS)
            offsets_high(t)
        for u in range(4):
            select("vs"[u % 2], t, u)
        spread(t)
        for i in range(16 - NS):
            c_some("vs"[i % 2], 1)
        c_dense(3)
        c_list(0, 2)
        for k in range(4):
            a_piece("v", k, 0, AV[k])
            a_piece("s", k, AV[k], 64)
            a_dense("DD", "d_d%d" % k, 0, k, k + 1)
            if k == 0:
                c_list(2, 4)
            if k == 2:
                d_send(t, 0)
        d_send(t, 1)
        if last:
            d_send(t, 2)
            d_send(t, 3)
            break
        di = "DI%d" % (t % 2)
        dmas("y", "d_i", [(T[di][:], T.AO[1::16, :])], pcs("AO"), [di])
        a_dense("DG", "d_g0", 2, 0, 4)
        const_round_v(t + 1)
        d_send(t, 2)
        d_send(t, 3)
        send("n%d" % t, T["IR%d" % t][:], T[di][:], [di], [("IR", t)], 1, "d_l2")
        const_round(t + 1)
        if t == 3:
            const_high()
        if t == RO - 2:
            last_list()

    for k in range(4):
        dmas("y", "d_out", [(T.yo[:, 64 * k:64 * k + 64], T.YR[:, 64 * k:64 * k + 64])], [("YR", k)], [])
    for sem, cnt in total.items():
        g.wait_ge(T.sem[sem], cnt)
